import numpy as np
import ml_dtypes


def mxq(x, axis, fmt="e4m3"):
    dtype, down = {"e4m3": (ml_dtypes.float8_e4m3fn, 7), "e5m2": (ml_dtypes.float8_e5m2, 14)}[fmt]
    v = np.moveaxis(np.asarray(x, np.float32).astype(ml_dtypes.bfloat16).astype(np.float64), axis, -1)
    blocks = v.reshape(v.shape[:-1] + (-1, 32))
    amax = np.abs(blocks).max(-1, keepdims=True)
    byte = np.maximum(np.where(amax > 0, np.frexp(amax)[1] - 1 + 127, 0) - down, 1)
    scale = np.exp2(byte - 127.0)
    codes = (blocks / scale).astype(np.float32).astype(dtype).astype(np.float64)
    return np.moveaxis((codes * scale).reshape(v.shape), -1, axis)


WIDE = False


def mx_kscale(k):
    if not WIDE:
        return np.ones(k)
    levels = np.array([10, -10, 5, -5, 0])
    if k % 512:
        return np.exp2(np.random.permutation(np.resize(levels, k // 32))).repeat(32)
    a = np.empty((k // 512, 16))
    for p in range(k // 512):
        a[p, :8] = np.random.permutation(np.resize(levels, 8))
        for g in range(8):
            far = levels[np.abs(levels - a[p, g]) >= 10]
            a[p, g + 8] = far[np.random.randint(len(far))]
    return np.exp2(a.ravel()).repeat(32)


BF16 = ml_dtypes.bfloat16


def bf(x):
    return np.asarray(x, np.float32).astype(BF16)


def f64(x):
    return np.asarray(x).astype(np.float64)


E2M1 = np.array([0.0, 0.5, 1.0, 1.5, 2.0, 3.0, 4.0, 6.0, -0.0, -0.5, -1.0, -1.5, -2.0, -3.0, -4.0, -6.0])


def pack_weight(w, fmt):
    k, n = w.shape
    w = f64(bf(w)).reshape(k // 32, 32, n)
    amax = np.abs(w).max(1)
    if fmt == "e4m3":
        byte = np.frexp(amax)[1] - 1 + 127 - 7
    else:
        mant, ex = np.frexp(amax / 6.0)
        byte = np.where(mant > 0.5, ex, ex - 1) + 127
    byte = np.clip(np.where(amax > 0, byte, 1), 1, 254)
    scaled = (w * np.exp2(127.0 - byte)[:, None, :]).reshape(k, n).astype(np.float32)
    by_word = np.ascontiguousarray(scaled.reshape(k // 512, 128, 4, n).transpose(0, 1, 3, 2))
    if fmt == "e4m3":
        words = by_word.astype(ml_dtypes.float8_e4m3fn).view(np.uint8)
    else:
        c = by_word.astype(ml_dtypes.float4_e2m1fn).view(np.uint8) & 0xF
        words = c[..., 0::2] | (c[..., 1::2] << 4)
    return np.ascontiguousarray(words), np.ascontiguousarray(byte.astype(np.uint8).reshape(k // 512, 16, n))


def unpack_weight(words, scales, fmt):
    g, p, n, _ = words.shape
    if fmt == "e4m3":
        vals = np.ascontiguousarray(words).view(ml_dtypes.float8_e4m3fn).astype(np.float64)
    else:
        nib = np.empty((g, p, n, 4), np.uint8)
        nib[..., 0::2] = words & 0xF
        nib[..., 1::2] = words >> 4
        vals = E2M1[nib]
    vals = vals * np.repeat(np.exp2(scales.astype(np.float64) - 127.0), 8, axis=1)[..., None]
    return vals.transpose(0, 1, 3, 2).reshape(g * 512, n)
def pack4(w):
    words, scales = pack_weight(w, "e2m1")
    return words.reshape(words.shape[0], 128, -1), scales


def unpack4(words, scales):
    return unpack_weight(words.reshape(words.shape[0], 128, -1, 2), scales, "e2m1")


M, KA, KB, D, R = 1024, 512, 1024, 2048, 512


def draw0():
    s, r, t = mx_kscale(KA), mx_kscale(KB), mx_kscale(D)
    b_words, b_scales = pack4(np.random.standard_normal((KB, D)) / np.sqrt(KA + KB) / r[:, None])
    c_words, c_scales = pack4(np.random.standard_normal((D, R)) / np.sqrt(D) / t[:, None])
    return {
        "xa": bf(np.random.standard_normal((M, KA)) * s),
        "xb": bf(np.random.standard_normal((M, KB)) * r),
        "a": bf(np.random.standard_normal((D, KA)) / np.sqrt(KA + KB) / s),
        "b_words": b_words,
        "b_scales": b_scales,
        "amp": bf((1 + 0.1 * np.random.standard_normal(D)) * t),
        "c_words": c_words,
        "c_scales": c_scales,
        "mean": bf(0.3 * np.random.standard_normal(R)),
    }


def core(xa, xb, a, b_words, b_scales, amp, c_words, c_scales, mean):
    b = unpack4(b_words, b_scales)
    c = unpack4(c_words, c_scales)
    lead = mxq(f64(xa), 1, "e4m3") @ mxq(f64(a), 1, "e4m3").T
    rest = mxq(f64(xb), 1, "e4m3") @ b
    z = lead + rest
    h = np.tanh(z) * f64(amp)
    y = (mxq(h, 1, "e4m3") @ c) + f64(mean)
    return y


def e4m3fn_bytes(y):
    return np.clip(np.asarray(y, np.float64), -448.0, 448.0).astype(np.float32).astype(ml_dtypes.float8_e4m3fn).view(np.uint8)


def e4m3fn_values(b):
    return np.asarray(b, np.uint8).view(ml_dtypes.float8_e4m3fn).astype(np.float64)


def setup_inputs():
    d = draw0()
    x0 = np.asarray(d['xb']).astype(np.float64)
    s = (np.max(np.abs(x0), axis=(0,), keepdims=True) / 448.0).astype(np.float32)
    out = {}
    for k, v in d.items():
        if k == 'xb':
            out['xb_bytes'] = e4m3fn_bytes(x0 / s.astype(np.float64))
            out['xb_scale'] = s
        else:
            out[k] = v
    return out


def reference(xa, xb_bytes, xb_scale, a, b_words, b_scales, amp, c_words, c_scales, mean):
    return core(xa, e4m3fn_values(xb_bytes) * xb_scale.astype(np.float64), a, b_words, b_scales, amp, c_words, c_scales, mean)

@@ -1,0 +1,287 @@
+from contextlib import ExitStack
+
+import concourse.mybir as mybir
+from concourse.masks import make_identity
+
+M, KA, KB, D, R = 1024, 512, 1024, 2048, 512
+FLOPS = 2 * M * D * (KA + KB) + 2 * M * D * R
+
+F32 = mybir.dt.float32
+BF16 = mybir.dt.bfloat16
+I32 = mybir.dt.int32
+U32 = mybir.dt.uint32
+U8 = mybir.dt.uint8
+FP8 = mybir.dt.float8_e4m3fn
+FP8X4 = mybir.dt.float8_e4m3fn_x4
+FP4X4 = mybir.dt.float4_e2m1fn_x4
+MULT = mybir.AluOpType.mult
+ADD = mybir.AluOpType.add
+TANH = mybir.ActivationFunctionType.Tanh
+
+P = 128
+T = 4
+W = 512
+HALF = W // 2
+GROUPS = D // W
+RANGES = M // W
+KPB = KB // W
+ORDER = [(0, 0), (0, 1), (1, 0), (0, 2), (1, 1), (0, 3), (1, 2), (1, 3)]
+
+
+def tile_projection_pursuit_responses_s3_kernel(
+    tc, xa, xb_bytes, xb_scale, a, b_words, b_scales, amp, c_words, c_scales, mean, out
+):
+    nc = tc.nc
+    with ExitStack() as ctx:
+        keep = ctx.enter_context(tc.tile_pool(name="keep", bufs=1))
+        work = ctx.enter_context(tc.tile_pool(name="work", bufs=3))
+        zpool = ctx.enter_context(tc.psum_pool(name="zpool", bufs=4))
+        tpool = ctx.enter_context(tc.psum_pool(name="tpool", bufs=2))
+        ypool = ctx.enter_context(tc.psum_pool(name="ypool", bufs=2))
+
+        a_rows = a.rearrange("(g p t) k -> g p t k", p=P, t=T)
+        xa_rows = xa.rearrange("(r p j) k -> r p j k", p=P, j=T)
+        xb_rows = xb_bytes.rearrange("(r p j) k -> r p j k", p=P, j=T)
+        out_rows = out.rearrange("(r p j) c -> r p j c", p=P, j=T)
+        bw_rows = b_words.bitcast(I32).rearrange("k p w -> p k w")
+        bs_rows = b_scales.bitcast(I32)
+        cw_rows = c_words.bitcast(I32).rearrange("k p w -> p k w")
+        cs_rows = c_scales.bitcast(I32)
+
+        scale_cols = keep.tile([P, 8], F32, name="scale_cols")
+        amp_b = keep.tile([P, GROUPS, T], BF16, name="amp_b")
+        amp_f = keep.tile([P, GROUPS, T, 4], F32, name="amp_f")
+        mean_sb = keep.tile([P, R], BF16, name="mean_sb")
+        bs_raw = keep.tile([P, KPB, D], U8, name="bs_raw")
+        cs = keep.tile([P, GROUPS, R], U8, align_bytes=64, name="cs")
+        cw = keep.tile([P, GROUPS, 2 * R], U8, align_bytes=64, name="cw")
+        bw_raw = [keep.tile([P, KPB, 2 * W], U8, name=f"bw_raw{g}") for g in range(GROUPS)]
+        a_raw = [keep.tile([P, T, KA], BF16, name=f"a_raw{g}") for g in range(GROUPS)]
+        xa_raw = [keep.tile([P, T, KA], BF16, name=f"xa_raw{r}") for r in range(RANGES)]
+        xb_raw = [keep.tile([P, T, KB], U8, name=f"xb_raw{r}") for r in range(RANGES)]
+
+        def load_bw(g):
+            nc.sync.dma_start(out=bw_raw[g][:].bitcast(I32), in_=bw_rows[:, :, g * 256 : (g + 1) * 256])
+
+        def load_a(g):
+            nc.sync.dma_start(out=a_raw[g][:], in_=a_rows[g])
+
+        def load_xa(r):
+            nc.sync.dma_start(out=xa_raw[r][:], in_=xa_rows[r])
+
+        def load_xb(r):
+            nc.sync.dma_start(out=xb_raw[r][:], in_=xb_rows[r])
+
+        nc.vector.memset(bs_raw[:].bitcast(I32), 0)
+        nc.gpsimd.memset(cs[:].bitcast(I32), 0)
+        nc.sync.dma_start(out=scale_cols[:], in_=xb_scale.rearrange("o (n m) -> n (o m)", m=8))
+        load_bw(0)
+        load_xb(0)
+        load_a(0)
+        load_xa(0)
+        for q in range(4):
+            nc.sync.dma_start(
+                out=bs_raw[q : P : 32].bitcast(I32),
+                in_=bs_rows[:, q : 16 : 4, :].rearrange("k s w -> s k w"),
+            )
+        nc.sync.dma_start(out=amp_b[:], in_=amp.rearrange("(g p t) -> p g t", p=P, t=T))
+        load_a(1)
+        load_bw(1)
+        load_xb(1)
+        load_xa(1)
+        load_a(2)
+        load_bw(2)
+        load_a(3)
+        load_bw(3)
+        nc.sync.dma_start(out=cw[:].bitcast(I32), in_=cw_rows)
+        for q in range(4):
+            nc.sync.dma_start(
+                out=cs[q : P : 32].bitcast(I32),
+                in_=cs_rows[:, q : 16 : 4, :].rearrange("k s w -> s k w"),
+            )
+        nc.sync.dma_start(out=mean_sb[:], in_=mean.partition_broadcast(P))
+
+        ident = keep.tile([P, P], F32, name="ident")
+        make_identity(nc, ident[:])
+        warm = keep.tile([P, 1], F32, name="warm")
+        nc.vector.memset(warm[:], 0.0)
+        warm_out = keep.tile([P, 1], F32, name="warm_out")
+        nc.scalar.activation(out=warm_out[:], in_=warm[:], func=TANH)
+
+        scale_rows = keep.tile([P, KB], F32, name="scale_rows")
+        for h in range(2):
+            sp = tpool.tile([P, W], F32, name="tr")
+            for m in range(4):
+                nc.tensor.transpose(
+                    sp[:, m * P : (m + 1) * P],
+                    scale_cols[:, 4 * h + m : 4 * h + m + 1].to_broadcast([P, P]),
+                    ident[:],
+                )
+            nc.scalar.copy(
+                out=scale_rows[:].rearrange("p (n m) -> p n m", m=8)[:, :, 4 * h : 4 * h + 4],
+                in_=sp[:].rearrange("p (m n) -> p n m", m=4),
+            )
+        nc.vector.tensor_copy(out=amp_f[:], in_=amp_b[:].unsqueeze(3).to_broadcast([P, GROUPS, T, 4]))
+
+        bw = {}
+        bs = {}
+        a_codes = {}
+        a_scales = {}
+        xa_codes = {}
+        xa_scales = {}
+        xb_codes = {}
+        xb_scales = {}
+        h_codes = {}
+        h_scales = {}
+
+        def permute_b(g):
+            bw[g] = keep.tile([P, KPB, 2 * W], U8, align_bytes=64, name=f"bw{g}")
+            bs[g] = keep.tile([P, KPB, W], U8, align_bytes=64, name=f"bs{g}")
+            for k in range(KPB):
+                nc.vector.tensor_copy(
+                    out=bw[g][:, k, :].rearrange("p (t q b) -> p t q b", t=T, b=2),
+                    in_=bw_raw[g][:, k, :].rearrange("p (q t b) -> p t q b", t=T, b=2),
+                )
+            nc.vector.tensor_copy(
+                out=bs[g][:].rearrange("p k (t q) -> p k t q", t=T),
+                in_=bs_raw[:, :, g * W : (g + 1) * W].rearrange("p k (q t) -> p k t q", t=T),
+            )
+
+        def quantize(name, grouped):
+            codes = keep.tile([P, W], U32, align_bytes=64, name=name + "_codes")
+            scales = keep.tile([P, W], U8, align_bytes=64, name=name + "_scales")
+            nc.vector.quantize_mx(out=codes[:].bitcast(FP8X4), scales=scales[:], in_=grouped)
+            return codes, scales
+
+        def turn_rows(raw, grouped):
+            words = raw[:].rearrange("p s k -> p (s k)").bitcast(F32)
+            gw = grouped[:].rearrange("p n t -> p (n t)").bitcast(F32)
+            for pair in range(2):
+                tr = tpool.tile([P, W], F32, name="tr")
+                for s in range(2):
+                    for u in range(2):
+                        c = (2 * pair + s) * 256
+                        o = (2 * s + u) * P
+                        nc.tensor.transpose(tr[:, o : o + P], words[:, c + u : c + 256 : 2], ident[:])
+                nc.scalar.copy(
+                    out=gw[:, pair * 512 : (pair + 1) * 512].rearrange("p (s r u) -> p s r u", s=2, u=2),
+                    in_=tr[:].rearrange("p (s u r) -> p s r u", s=2, u=2),
+                )
+
+        def prepare_a(g):
+            grouped = work.tile([P, W, T], BF16, align_bytes=64, name="grouped")
+            turn_rows(a_raw[g], grouped)
+            a_codes[g], a_scales[g] = quantize(f"a{g}", grouped[:].rearrange("p n t -> p (n t)"))
+
+        def prepare_xa(r):
+            grouped = work.tile([P, W, T], BF16, align_bytes=64, name="grouped")
+            turn_rows(xa_raw[r], grouped)
+            xa_codes[r], xa_scales[r] = quantize(f"xa{r}", grouped[:].rearrange("p n t -> p (n t)"))
+
+        def prepare_xb(r):
+            grouped = work.tile([P, KPB, W * T], BF16, align_bytes=64, name="grouped_xb")
+            gw = grouped[:].rearrange("p k n -> p (k n)").bitcast(F32).rearrange("p (k n) -> p k n", k=KPB)
+            for j in range(T):
+                val = work.tile([P, KB], BF16, name="xb_val")
+                nc.vector.tensor_tensor(out=val[:], in0=xb_raw[r][:, j, :].bitcast(FP8), in1=scale_rows[:], op=MULT)
+                words = val[:].bitcast(F32)
+                tr = tpool.tile([P, W], F32, name="tr")
+                for k in range(KPB):
+                    for u in range(2):
+                        o = (2 * k + u) * P
+                        nc.tensor.transpose(tr[:, o : o + P], words[:, 256 * k + u : 256 * (k + 1) : 2], ident[:])
+                nc.scalar.copy(
+                    out=gw[:, :, j * 256 : (j + 1) * 256].rearrange("p k (r u) -> p k r u", u=2),
+                    in_=tr[:].rearrange("p (k u r) -> p k r u", k=KPB, u=2),
+                )
+            for k in range(KPB):
+                xb_codes[r, k], xb_scales[r, k] = quantize(f"xb{r}{k}", grouped[:, k, :])
+
+        def project(r, g):
+            th = work.tile([P, T, W], F32, name="th")
+            for t in range(T):
+                cols = slice(t * P, (t + 1) * P)
+                z = zpool.tile([P, W], F32, name="z")
+                nc.tensor.matmul_mx(
+                    out=z[:],
+                    lhsT=a_codes[g][:, cols].bitcast(FP8X4),
+                    lhsT_scale=a_scales[g][:, cols],
+                    rhs=xa_codes[r][:].bitcast(FP8X4),
+                    rhs_scale=xa_scales[r][:],
+                    start=True,
+                    stop=False,
+                )
+                for k in range(KPB):
+                    nc.tensor.matmul_mx(
+                        out=z[:],
+                        lhsT=bw[g][:, k, t * 256 : (t + 1) * 256].bitcast(FP4X4),
+                        lhsT_scale=bs[g][:, k, cols],
+                        rhs=xb_codes[r, k][:].bitcast(FP8X4),
+                        rhs_scale=xb_scales[r, k][:],
+                        start=False,
+                        stop=(k == KPB - 1),
+                    )
+                nc.scalar.activation(out=th[:, t, :], in_=z[:], func=TANH)
+            return th
+
+        def ridge(r, g, th):
+            hb = work.tile([P, W, T], BF16, align_bytes=64, name="hb")
+            codes = keep.tile([P, W], U32, align_bytes=64, name=f"h{r}{g}_codes")
+            scales = keep.tile([P, W], U8, align_bytes=64, name=f"h{r}{g}_scales")
+            for h in range(2):
+                cols = slice(h * HALF, (h + 1) * HALF)
+                nc.vector.tensor_tensor(
+                    out=hb[:, cols, :].rearrange("p (c i) t -> p c t i", i=4),
+                    in0=th[:, :, cols].rearrange("p t (c i) -> p c t i", i=4),
+                    in1=amp_f[:, g, :, :].unsqueeze(1).to_broadcast([P, HALF // 4, T, 4]),
+                    op=MULT,
+                )
+            for h in range(2):
+                cols = slice(h * HALF, (h + 1) * HALF)
+                nc.vector.quantize_mx(
+                    out=codes[:, cols].bitcast(FP8X4),
+                    scales=scales[:, cols],
+                    in_=hb[:, cols, :].rearrange("p n t -> p (n t)"),
+                )
+            h_codes[r, g] = codes
+            h_scales[r, g] = scales
+
+        def respond(r, spare):
+            for j in range(T):
+                cols = slice(j * P, (j + 1) * P)
+                if spare and j >= 2:
+                    y = tpool.tile([P, W], F32, name="tr")
+                else:
+                    y = ypool.tile([P, W], F32, name="y")
+                for g in range(GROUPS):
+                    nc.tensor.matmul_mx(
+                        out=y[:],
+                        lhsT=h_codes[r, g][:, cols].bitcast(FP8X4),
+                        lhsT_scale=h_scales[r, g][:, cols],
+                        rhs=cw[:, g, :].bitcast(FP4X4),
+                        rhs_scale=cs[:, g, :],
+                        start=(g == 0),
+                        stop=(g == GROUPS - 1),
+                    )
+                ysb = work.tile([P, R], F32, name="ysb")
+                nc.vector.tensor_tensor(out=ysb[:], in0=y[:], in1=mean_sb[:], op=ADD)
+                nc.sync.dma_start(out=out_rows[r][:, j, :], in_=ysb[:])
+
+        permute_b(0)
+        prepare_a(0)
+        prepare_xa(0)
+        prepare_xb(0)
+        prep = {
+            (0, 0): lambda: (permute_b(1), prepare_a(1)),
+            (0, 1): lambda: (prepare_xa(1), prepare_xb(1)),
+            (1, 0): lambda: (permute_b(2), prepare_a(2)),
+            (1, 1): lambda: (permute_b(3), prepare_a(3)),
+        }
+        for r, g in ORDER:
+            th = project(r, g)
+            if (r, g) in prep:
+                prep[r, g]()
+            ridge(r, g, th)
+            if (r, g) == (0, 3):
+                respond(0, False)
+        respond(1, True)

@@ -16,6 +16,7 @@ FP8X4 = mybir.dt.float8_e4m3fn_x4
 FP4X4 = mybir.dt.float4_e2m1fn_x4
 MULT = mybir.AluOpType.mult
 ADD = mybir.AluOpType.add
+COPY = mybir.ActivationFunctionType.Copy
 TANH = mybir.ActivationFunctionType.Tanh
 
 P = 128
@@ -25,7 +26,37 @@ HALF = W // 2
 GROUPS = D // W
 RANGES = M // W
 KPB = KB // W
-ORDER = [(0, 0), (0, 1), (1, 0), (0, 2), (1, 1), (0, 3), (1, 2), (1, 3)]
+SCALAR_UNITS = ()
+SEQ = """
+permw0 trs0 trs1 cps0 cps1 deq00 tra0.0 tra0.1 cpa0.0 deq01 cpa0.1 trxb00 
+trxa0.0 deq02 cpxb00 cpxa0.0 trxb01 deq03 trxb02 cpxb01 cpxb02 trxa0.1 perms0 trxb03 
+qa0 cpxa0.1 permw1 cpxb03 tra1.0 tra1.1 cpa1.0 qxa0 cpa1.1 tra2.0 qxb0 tra2.1 
+cpa2.0 Z00.0 cpa2.1 perms1 qa1 Z00.1 tanh00.0 permw2 Z00.2 tanh00.1 perms2 Z00.3 
+tanh00.2 qa2 Z01.0 tanh00.3 deq10 Z01.1 tanh01.0 mul00.0 Z01.2 tanh01.1 mul00.1 Z01.3 
+tanh01.2 trxb10 tanh01.3 qh00.0 qh00.1 trxa1.0 cpxb10 deq11 Z02.0 cpxa1.0 mul01.0 trxa1.1 
+tanh02.0 trxb11 cpxa1.1 mul01.1 Z02.1 cpxb11 qxa1 Z02.2 tanh02.1 qh01.0 qh01.1 Z02.3 
+tanh02.2 permw3 tra3.0 tanh02.3 perms3 tra3.1 cpa3.0 deq12 Y00.0 cpa3.1 Y01.0 Y00.1 
+Y01.1 qa3 trxb12 deq13 Z03.0 cpxb12 mul02.0 Z03.1 tanh03.0 trxb13 tanh03.1 mul02.1 
+Z03.2 cpxb13 qxb1 Z03.3 tanh03.2 Z10.0 tanh03.3 qh02.0 qh02.1 mul03.0 Z10.1 tanh10.0 
+Z10.2 tanh10.1 mul03.1 Z10.3 tanh10.2 qh03.0 qh03.1 Y00.2 tanh10.3 Y01.2 Y00.3 Y01.3 
+mul10.0 Z11.0 Z11.1 mul10.1 tanh11.0 Z11.2 tanh11.1 qh10.0 qh10.1 Z11.3 mean00 tanh11.2 
+mean01 Y02.0 tanh11.3 Z12.0 mul11.0 Y02.1 tanh12.0 Y03.0 Y02.2 Y03.1 mul11.1 Y02.3 
+Y03.2 Z12.1 mean02 Y03.3 qh11.0 tanh12.1 Z12.2 mean03 qh11.1 Z12.3 tanh12.2 Z13.0 
+tanh12.3 Z13.1 mul12.0 tanh13.0 Z13.2 tanh13.1 mul12.1 Z13.3 tanh13.2 qh12.0 Y10.0 qh12.1 
+tanh13.3 Y11.0 Y12.0 Y13.0 mul13.0 Y10.1 Y11.1 Y12.1 Y13.1 mul13.1 Y10.2 Y11.2 
+Y12.2
+Y13.2
+qh13.0
+qh13.1
+Y10.3
+Y11.3
+mean10
+Y12.3
+Y13.3
+mean11
+mean12
+mean13
+"""
 
 
 def tile_projection_pursuit_responses_s3_kernel(
@@ -109,179 +140,223 @@ def tile_projection_pursuit_responses_s3_kernel(
         nc.scalar.activation(out=warm_out[:], in_=warm[:], func=TANH)
 
         scale_rows = keep.tile([P, KB], F32, name="scale_rows")
-        for h in range(2):
-            sp = tpool.tile([P, W], F32, name="tr")
+        nc.vector.tensor_copy(out=amp_f[:], in_=amp_b[:].unsqueeze(3).to_broadcast([P, GROUPS, T, 4]))
+        live = {}
+        codes = {}
+        scales = {}
+        for g in range(GROUPS):
+            live["bw", g] = keep.tile([P, KPB, 2 * W], U8, align_bytes=64, name=f"bw{g}")
+            live["bs", g] = keep.tile([P, KPB, W], U8, align_bytes=64, name=f"bs{g}")
+
+        def trs(h):
+            live["sp", h] = tpool.tile([P, W], F32, name="tr")
             for m in range(4):
                 nc.tensor.transpose(
-                    sp[:, m * P : (m + 1) * P],
+                    live["sp", h][:, m * P : (m + 1) * P],
                     scale_cols[:, 4 * h + m : 4 * h + m + 1].to_broadcast([P, P]),
                     ident[:],
                 )
+
+        def cps(h):
             nc.scalar.copy(
                 out=scale_rows[:].rearrange("p (n m) -> p n m", m=8)[:, :, 4 * h : 4 * h + 4],
-                in_=sp[:].rearrange("p (m n) -> p n m", m=4),
+                in_=live["sp", h][:].rearrange("p (m n) -> p n m", m=4),
             )
-        nc.vector.tensor_copy(out=amp_f[:], in_=amp_b[:].unsqueeze(3).to_broadcast([P, GROUPS, T, 4]))
 
-        bw = {}
-        bs = {}
-        a_codes = {}
-        a_scales = {}
-        xa_codes = {}
-        xa_scales = {}
-        xb_codes = {}
-        xb_scales = {}
-        h_codes = {}
-        h_scales = {}
-
-        def permute_b(g):
-            bw[g] = keep.tile([P, KPB, 2 * W], U8, align_bytes=64, name=f"bw{g}")
-            bs[g] = keep.tile([P, KPB, W], U8, align_bytes=64, name=f"bs{g}")
+        def permw(g):
             for k in range(KPB):
                 nc.vector.tensor_copy(
-                    out=bw[g][:, k, :].rearrange("p (t q b) -> p t q b", t=T, b=2),
+                    out=live["bw", g][:, k, :].rearrange("p (t q b) -> p t q b", t=T, b=2),
                     in_=bw_raw[g][:, k, :].rearrange("p (q t b) -> p t q b", t=T, b=2),
                 )
+
+        def perms(g):
             nc.vector.tensor_copy(
-                out=bs[g][:].rearrange("p k (t q) -> p k t q", t=T),
+                out=live["bs", g][:].rearrange("p k (t q) -> p k t q", t=T),
                 in_=bs_raw[:, :, g * W : (g + 1) * W].rearrange("p k (q t) -> p k t q", t=T),
             )
 
-        def quantize(name, grouped):
-            codes = keep.tile([P, W], U32, align_bytes=64, name=name + "_codes")
-            scales = keep.tile([P, W], U8, align_bytes=64, name=name + "_scales")
-            nc.vector.quantize_mx(out=codes[:].bitcast(FP8X4), scales=scales[:], in_=grouped)
-            return codes, scales
+        def quantize(key, grouped):
+            codes[key] = keep.tile([P, W], U32, align_bytes=64, name=key + "_codes")
+            scales[key] = keep.tile([P, W], U8, align_bytes=64, name=key + "_scales")
+            nc.vector.quantize_mx(out=codes[key][:].bitcast(FP8X4), scales=scales[key][:], in_=grouped)
 
-        def turn_rows(raw, grouped):
-            words = raw[:].rearrange("p s k -> p (s k)").bitcast(F32)
-            gw = grouped[:].rearrange("p n t -> p (n t)").bitcast(F32)
-            for pair in range(2):
-                tr = tpool.tile([P, W], F32, name="tr")
-                for s in range(2):
-                    for u in range(2):
-                        c = (2 * pair + s) * 256
-                        o = (2 * s + u) * P
-                        nc.tensor.transpose(tr[:, o : o + P], words[:, c + u : c + 256 : 2], ident[:])
-                nc.scalar.copy(
-                    out=gw[:, pair * 512 : (pair + 1) * 512].rearrange("p (s r u) -> p s r u", s=2, u=2),
-                    in_=tr[:].rearrange("p (s u r) -> p s r u", s=2, u=2),
-                )
+        raws = {}
+        for g in range(GROUPS):
+            raws[f"a{g}"] = a_raw[g]
+        for r in range(RANGES):
+            raws[f"xa{r}"] = xa_raw[r]
 
-        def prepare_a(g):
-            grouped = work.tile([P, W, T], BF16, align_bytes=64, name="grouped")
-            turn_rows(a_raw[g], grouped)
-            a_codes[g], a_scales[g] = quantize(f"a{g}", grouped[:].rearrange("p n t -> p (n t)"))
+        def tr_rows(key, pair):
+            words = raws[key][:].rearrange("p s k -> p (s k)").bitcast(F32)
+            live["tr", key, pair] = tpool.tile([P, W], F32, name="tr")
+            for s in range(2):
+                for u in range(2):
+                    c = (2 * pair + s) * 256
+                    o = (2 * s + u) * P
+                    nc.tensor.transpose(
+                        live["tr", key, pair][:, o : o + P], words[:, c + u : c + 256 : 2], ident[:]
+                    )
 
-        def prepare_xa(r):
-            grouped = work.tile([P, W, T], BF16, align_bytes=64, name="grouped")
-            turn_rows(xa_raw[r], grouped)
-            xa_codes[r], xa_scales[r] = quantize(f"xa{r}", grouped[:].rearrange("p n t -> p (n t)"))
+        def cp_rows(key, pair):
+            if ("grouped", key) not in live:
+                live["grouped", key] = work.tile([P, W, T], BF16, align_bytes=64, name="grouped")
+            gw = live["grouped", key][:].rearrange("p n t -> p (n t)").bitcast(F32)
+            nc.scalar.copy(
+                out=gw[:, pair * 512 : (pair + 1) * 512].rearrange("p (s r u) -> p s r u", s=2, u=2),
+                in_=live["tr", key, pair][:].rearrange("p (s u r) -> p s r u", s=2, u=2),
+            )
 
-        def prepare_xb(r):
-            grouped = work.tile([P, KPB, W * T], BF16, align_bytes=64, name="grouped_xb")
-            gw = grouped[:].rearrange("p k n -> p (k n)").bitcast(F32).rearrange("p (k n) -> p k n", k=KPB)
-            for j in range(T):
-                val = work.tile([P, KB], BF16, name="xb_val")
-                nc.vector.tensor_tensor(out=val[:], in0=xb_raw[r][:, j, :].bitcast(FP8), in1=scale_rows[:], op=MULT)
-                words = val[:].bitcast(F32)
-                tr = tpool.tile([P, W], F32, name="tr")
-                for k in range(KPB):
-                    for u in range(2):
-                        o = (2 * k + u) * P
-                        nc.tensor.transpose(tr[:, o : o + P], words[:, 256 * k + u : 256 * (k + 1) : 2], ident[:])
-                nc.scalar.copy(
-                    out=gw[:, :, j * 256 : (j + 1) * 256].rearrange("p k (r u) -> p k r u", u=2),
-                    in_=tr[:].rearrange("p (k u r) -> p k r u", k=KPB, u=2),
-                )
+        def q_rows(key):
+            quantize(key, live["grouped", key][:].rearrange("p n t -> p (n t)"))
+
+        def deq(r, j):
+            live["val", r, j] = work.tile([P, KB], BF16, name="xb_val")
+            nc.vector.tensor_tensor(
+                out=live["val", r, j][:], in0=xb_raw[r][:, j, :].bitcast(FP8), in1=scale_rows[:], op=MULT
+            )
+
+        def trxb(r, j):
+            words = live["val", r, j][:].bitcast(F32)
+            live["trx", r, j] = tpool.tile([P, W], F32, name="tr")
             for k in range(KPB):
-                xb_codes[r, k], xb_scales[r, k] = quantize(f"xb{r}{k}", grouped[:, k, :])
+                for u in range(2):
+                    o = (2 * k + u) * P
+                    nc.tensor.transpose(
+                        live["trx", r, j][:, o : o + P], words[:, 256 * k + u : 256 * (k + 1) : 2], ident[:]
+                    )
 
-        def project(r, g):
-            th = work.tile([P, T, W], F32, name="th")
-            for t in range(T):
-                cols = slice(t * P, (t + 1) * P)
-                z = zpool.tile([P, W], F32, name="z")
+        def cpxb(r, j):
+            if ("gx", r) not in live:
+                live["gx", r] = work.tile([P, KPB, W * T], BF16, align_bytes=64, name="grouped_xb")
+            gw = live["gx", r][:].rearrange("p k n -> p (k n)").bitcast(F32).rearrange("p (k n) -> p k n", k=KPB)
+            nc.scalar.copy(
+                out=gw[:, :, j * 256 : (j + 1) * 256].rearrange("p k (r u) -> p k r u", u=2),
+                in_=live["trx", r, j][:].rearrange("p (k u r) -> p k r u", k=KPB, u=2),
+            )
+
+        def qxb(r):
+            for k in range(KPB):
+                quantize(f"xb{r}{k}", live["gx", r][:, k, :])
+
+        def project(r, g, t):
+            cols = slice(t * P, (t + 1) * P)
+            z = zpool.tile([P, W], F32, name="z")
+            live["z", r, g, t] = z
+            nc.tensor.matmul_mx(
+                out=z[:],
+                lhsT=codes[f"a{g}"][:, cols].bitcast(FP8X4),
+                lhsT_scale=scales[f"a{g}"][:, cols],
+                rhs=codes[f"xa{r}"][:].bitcast(FP8X4),
+                rhs_scale=scales[f"xa{r}"][:],
+                start=True,
+                stop=False,
+            )
+            for k in range(KPB):
                 nc.tensor.matmul_mx(
                     out=z[:],
-                    lhsT=a_codes[g][:, cols].bitcast(FP8X4),
-                    lhsT_scale=a_scales[g][:, cols],
-                    rhs=xa_codes[r][:].bitcast(FP8X4),
-                    rhs_scale=xa_scales[r][:],
-                    start=True,
-                    stop=False,
+                    lhsT=live["bw", g][:, k, t * 256 : (t + 1) * 256].bitcast(FP4X4),
+                    lhsT_scale=live["bs", g][:, k, cols],
+                    rhs=codes[f"xb{r}{k}"][:].bitcast(FP8X4),
+                    rhs_scale=scales[f"xb{r}{k}"][:],
+                    start=False,
+                    stop=(k == KPB - 1),
                 )
-                for k in range(KPB):
-                    nc.tensor.matmul_mx(
-                        out=z[:],
-                        lhsT=bw[g][:, k, t * 256 : (t + 1) * 256].bitcast(FP4X4),
-                        lhsT_scale=bs[g][:, k, cols],
-                        rhs=xb_codes[r, k][:].bitcast(FP8X4),
-                        rhs_scale=xb_scales[r, k][:],
-                        start=False,
-                        stop=(k == KPB - 1),
-                    )
-                nc.scalar.activation(out=th[:, t, :], in_=z[:], func=TANH)
-            return th
 
-        def ridge(r, g, th):
-            hb = work.tile([P, W, T], BF16, align_bytes=64, name="hb")
-            codes = keep.tile([P, W], U32, align_bytes=64, name=f"h{r}{g}_codes")
-            scales = keep.tile([P, W], U8, align_bytes=64, name=f"h{r}{g}_scales")
-            for h in range(2):
-                cols = slice(h * HALF, (h + 1) * HALF)
+        def tanh(r, g, t):
+            if ("th", r, g) not in live:
+                live["th", r, g] = work.tile([P, T, W], F32, name="th")
+            nc.scalar.activation(out=live["th", r, g][:, t, :], in_=live["z", r, g, t][:], func=TANH)
+
+        def smul(r, g, t):
+            if ("hp", r, g) not in live:
+                live["hp", r, g] = work.tile([P, T, W], BF16, name="hp")
+            nc.scalar.activation(
+                out=live["hp", r, g][:, t, :], in_=live["th", r, g][:, t, :], func=COPY, scale=amp_f[:, g, t, 0:1]
+            )
+
+        def mul(r, g, h):
+            if h == 0:
+                live["hb", r, g] = work.tile([P, W, T], BF16, align_bytes=64, name="hb")
+            cols = slice(h * HALF, (h + 1) * HALF)
+            dst = live["hb", r, g][:, cols, :].rearrange("p (c i) t -> p c t i", i=4)
+            if (r, g) in SCALAR_UNITS:
+                nc.vector.tensor_copy(out=dst, in_=live["hp", r, g][:, :, cols].rearrange("p t (c i) -> p c t i", i=4))
+            else:
                 nc.vector.tensor_tensor(
-                    out=hb[:, cols, :].rearrange("p (c i) t -> p c t i", i=4),
-                    in0=th[:, :, cols].rearrange("p t (c i) -> p c t i", i=4),
+                    out=dst,
+                    in0=live["th", r, g][:, :, cols].rearrange("p t (c i) -> p c t i", i=4),
                     in1=amp_f[:, g, :, :].unsqueeze(1).to_broadcast([P, HALF // 4, T, 4]),
                     op=MULT,
                 )
-            for h in range(2):
-                cols = slice(h * HALF, (h + 1) * HALF)
-                nc.vector.quantize_mx(
-                    out=codes[:, cols].bitcast(FP8X4),
-                    scales=scales[:, cols],
-                    in_=hb[:, cols, :].rearrange("p n t -> p (n t)"),
-                )
-            h_codes[r, g] = codes
-            h_scales[r, g] = scales
 
-        def respond(r, spare):
-            for j in range(T):
-                cols = slice(j * P, (j + 1) * P)
-                if spare and j >= 2:
-                    y = tpool.tile([P, W], F32, name="tr")
+        def qh(r, g, h):
+            key = f"h{r}{g}"
+            if h == 0:
+                codes[key] = keep.tile([P, W], U32, align_bytes=64, name=key + "_codes")
+                scales[key] = keep.tile([P, W], U8, align_bytes=64, name=key + "_scales")
+            cols = slice(h * HALF, (h + 1) * HALF)
+            nc.vector.quantize_mx(
+                out=codes[key][:, cols].bitcast(FP8X4),
+                scales=scales[key][:, cols],
+                in_=live["hb", r, g][:, cols, :].rearrange("p n t -> p (n t)"),
+            )
+
+        def respond(r, j, g):
+            if ("y", r, j) not in live:
+                if r == 1 and j >= 2:
+                    live["y", r, j] = tpool.tile([P, W], F32, name="tr")
                 else:
-                    y = ypool.tile([P, W], F32, name="y")
-                for g in range(GROUPS):
-                    nc.tensor.matmul_mx(
-                        out=y[:],
-                        lhsT=h_codes[r, g][:, cols].bitcast(FP8X4),
-                        lhsT_scale=h_scales[r, g][:, cols],
-                        rhs=cw[:, g, :].bitcast(FP4X4),
-                        rhs_scale=cs[:, g, :],
-                        start=(g == 0),
-                        stop=(g == GROUPS - 1),
-                    )
-                ysb = work.tile([P, R], F32, name="ysb")
-                nc.vector.tensor_tensor(out=ysb[:], in0=y[:], in1=mean_sb[:], op=ADD)
-                nc.sync.dma_start(out=out_rows[r][:, j, :], in_=ysb[:])
+                    live["y", r, j] = ypool.tile([P, W], F32, name="y")
+                live["n", r, j] = 0
+            key = f"h{r}{g}"
+            cols = slice(j * P, (j + 1) * P)
+            n = live["n", r, j]
+            nc.tensor.matmul_mx(
+                out=live["y", r, j][:],
+                lhsT=codes[key][:, cols].bitcast(FP8X4),
+                lhsT_scale=scales[key][:, cols],
+                rhs=cw[:, g, :].bitcast(FP4X4),
+                rhs_scale=cs[:, g, :],
+                start=(n == 0),
+                stop=(n == GROUPS - 1),
+            )
+            live["n", r, j] = n + 1
 
-        permute_b(0)
-        prepare_a(0)
-        prepare_xa(0)
-        prepare_xb(0)
-        prep = {
-            (0, 0): lambda: (permute_b(1), prepare_a(1)),
-            (0, 1): lambda: (prepare_xa(1), prepare_xb(1)),
-            (1, 0): lambda: (permute_b(2), prepare_a(2)),
-            (1, 1): lambda: (permute_b(3), prepare_a(3)),
-        }
-        for r, g in ORDER:
-            th = project(r, g)
-            if (r, g) in prep:
-                prep[r, g]()
-            ridge(r, g, th)
-            if (r, g) == (0, 3):
-                respond(0, False)
-        respond(1, True)
+        def add_mean(r, j):
+            ysb = work.tile([P, R], F32, name="ysb")
+            nc.vector.tensor_tensor(out=ysb[:], in0=live["y", r, j][:], in1=mean_sb[:], op=ADD)
+            nc.sync.dma_start(out=out_rows[r][:, j, :], in_=ysb[:])
+
+        table = {}
+        for h in range(2):
+            table[f"trs{h}"] = (trs, h)
+            table[f"cps{h}"] = (cps, h)
+        for g in range(GROUPS):
+            table[f"permw{g}"] = (permw, g)
+            table[f"perms{g}"] = (perms, g)
+        for key in raws:
+            for pair in range(2):
+                table[f"tr{key}.{pair}"] = (tr_rows, key, pair)
+                table[f"cp{key}.{pair}"] = (cp_rows, key, pair)
+            table[f"q{key}"] = (q_rows, key)
+        for r in range(RANGES):
+            table[f"qxb{r}"] = (qxb, r)
+            for j in range(T):
+                table[f"deq{r}{j}"] = (deq, r, j)
+                table[f"trxb{r}{j}"] = (trxb, r, j)
+                table[f"cpxb{r}{j}"] = (cpxb, r, j)
+                table[f"mean{r}{j}"] = (add_mean, r, j)
+                for g in range(GROUPS):
+                    table[f"Y{r}{j}.{g}"] = (respond, r, j, g)
+                    table[f"Z{r}{g}.{j}"] = (project, r, g, j)
+                    table[f"tanh{r}{g}.{j}"] = (tanh, r, g, j)
+                    table[f"smul{r}{g}.{j}"] = (smul, r, g, j)
+            for g in range(GROUPS):
+                for h in range(2):
+                    table[f"mul{r}{g}.{h}"] = (mul, r, g, h)
+                    table[f"qh{r}{g}.{h}"] = (qh, r, g, h)
+        with tc.manual_schedule():
+            for name in SEQ.split():
+                job = table[name]
+                job[0](*job[1:])

@@ -21,42 +21,32 @@ TANH = mybir.ActivationFunctionType.Tanh
 
 P = 128
 T = 4
+SEQ = """
+permw0 trs0 cps0 trs1 cps1 tra0.0 cpa0.0 tra0.1 cpa0.1 trxa0.0 cpxa0.0 trxa0.1
+cpxa0.1 deq00 trxb00 cpxb00 deq01 deq02 trxb01 cpxb01 deq03 trxb02 cpxb02 trxb03
+cpxb03 perms0 tra2.0 cpa2.0 tra2.1 cpa2.1 tra1.0 cpa1.0 tra1.1 cpa1.1 qa0 perms1
+tra3.0 cpa3.0 qxa0 deq10 qxb0 trxb10 cpxb10 L00.0 L00.1 L00.2 L00.3 tra3.1
+cpa3.1 deq11 trxb11 cpxb11 permw1 qa1 Z00.0 tanh00.0 Z00.1 tanh00.1 perms2 qa2
+deq12 qa3 Z00.2 tanh00.2 Z00.3 tanh00.3 L01.0 Z01.0 tanh01.0 L01.1 Z01.1 tanh01.1
+permw2 L01.2 Z01.2 tanh01.2 L01.3 Z01.3 tanh01.3 trxa1.0 cpxa1.0 trxa1.1 cpxa1.1 permw3
+perms3 mul00 deq13 L02.0 Z02.0 tanh02.0 L02.1 Z02.1 tanh02.1 L02.2 Z02.2 tanh02.2
+L02.3 Z02.3 tanh02.3 qxa1 trxb12 cpxb12 trxb13 cpxb13 mul01 qxb1 mul02 L03.0
+Z03.0 tanh03.0 L03.1 Z03.1 tanh03.1 L03.2 Z03.2 tanh03.2 L03.3 Z03.3 tanh03.3 qh00
+mul03 L10.0 Z10.0 tanh10.0 L10.1 Z10.1 tanh10.1 L10.2 Z10.2 tanh10.2 L10.3 Z10.3
+tanh10.3 qh02 L11.0 Z11.0 tanh11.0 L11.1 Z11.1 tanh11.1 L11.2 Z11.2 tanh11.2 L11.3
+Z11.3 tanh11.3 qh03 mul10 qh01 qh10 L12.0 Z12.0 tanh12.0 L12.1 Z12.1 tanh12.1
+L12.2 Z12.2 tanh12.2 L12.3 Z12.3 tanh12.3 mul11 YE00 L13.0 Z13.0 tanh13.0 L13.1
+Z13.1 tanh13.1 L13.2 Z13.2 tanh13.2 L13.3 Z13.3 tanh13.3 YL00 mul12 qh11 qh12
+YE01 YL01 YE02 YL02 mean00 mean01 mul13.0 mean02 qh13.0 YE03 YL03 mean03
+mul13.1 qh13.1 YE10 YL10 mean10 YE11 YL11 mean11 YE12 YL12 mean12 YE13
+YL13
+mean13
+"""
 W = 512
 HALF = W // 2
 GROUPS = D // W
 RANGES = M // W
 KPB = KB // W
-SCALAR_UNITS = ()
-SEQ = """
-permw0 trs0 trs1 cps0 cps1 deq00 tra0.0 tra0.1 cpa0.0 deq01 cpa0.1 trxb00 
-trxa0.0 deq02 cpxb00 cpxa0.0 trxb01 deq03 trxb02 cpxb01 cpxb02 trxa0.1 perms0 trxb03 
-qa0 cpxa0.1 permw1 cpxb03 tra1.0 tra1.1 cpa1.0 qxa0 cpa1.1 tra2.0 qxb0 tra2.1 
-cpa2.0 Z00.0 cpa2.1 perms1 qa1 Z00.1 tanh00.0 permw2 Z00.2 tanh00.1 perms2 Z00.3 
-tanh00.2 qa2 Z01.0 tanh00.3 deq10 Z01.1 tanh01.0 mul00.0 Z01.2 tanh01.1 mul00.1 Z01.3 
-tanh01.2 trxb10 tanh01.3 qh00.0 qh00.1 trxa1.0 cpxb10 deq11 Z02.0 cpxa1.0 mul01.0 trxa1.1 
-tanh02.0 trxb11 cpxa1.1 mul01.1 Z02.1 cpxb11 qxa1 Z02.2 tanh02.1 qh01.0 qh01.1 Z02.3 
-tanh02.2 permw3 tra3.0 tanh02.3 perms3 tra3.1 cpa3.0 deq12 Y00.0 cpa3.1 Y01.0 Y00.1 
-Y01.1 qa3 trxb12 deq13 Z03.0 cpxb12 mul02.0 Z03.1 tanh03.0 trxb13 tanh03.1 mul02.1 
-Z03.2 cpxb13 qxb1 Z03.3 tanh03.2 Z10.0 tanh03.3 qh02.0 qh02.1 mul03.0 Z10.1 tanh10.0 
-Z10.2 tanh10.1 mul03.1 Z10.3 tanh10.2 qh03.0 qh03.1 Y00.2 tanh10.3 Y01.2 Y00.3 Y01.3 
-mul10.0 Z11.0 Z11.1 mul10.1 tanh11.0 Z11.2 tanh11.1 qh10.0 qh10.1 Z11.3 mean00 tanh11.2 
-mean01 Y02.0 tanh11.3 Z12.0 mul11.0 Y02.1 tanh12.0 Y03.0 Y02.2 Y03.1 mul11.1 Y02.3 
-Y03.2 Z12.1 mean02 Y03.3 qh11.0 tanh12.1 Z12.2 mean03 qh11.1 Z12.3 tanh12.2 Z13.0 
-tanh12.3 Z13.1 mul12.0 tanh13.0 Z13.2 tanh13.1 mul12.1 Z13.3 tanh13.2 qh12.0 Y10.0 qh12.1 
-tanh13.3 Y11.0 Y12.0 Y13.0 mul13.0 Y10.1 Y11.1 Y12.1 Y13.1 mul13.1 Y10.2 Y11.2 
-Y12.2
-Y13.2
-qh13.0
-qh13.1
-Y10.3
-Y11.3
-mean10
-Y12.3
-Y13.3
-mean11
-mean12
-mean13
-"""
 
 
 def tile_projection_pursuit_responses_s3_kernel(
@@ -65,7 +55,7 @@ def tile_projection_pursuit_responses_s3_kernel(
     nc = tc.nc
     with ExitStack() as ctx:
         keep = ctx.enter_context(tc.tile_pool(name="keep", bufs=1))
-        work = ctx.enter_context(tc.tile_pool(name="work", bufs=3))
+        work = ctx.enter_context(tc.tile_pool(name="work", bufs=4))
         zpool = ctx.enter_context(tc.psum_pool(name="zpool", bufs=4))
         tpool = ctx.enter_context(tc.psum_pool(name="tpool", bufs=2))
         ypool = ctx.enter_context(tc.psum_pool(name="ypool", bufs=2))
@@ -115,15 +105,15 @@ def tile_projection_pursuit_responses_s3_kernel(
                 out=bs_raw[q : P : 32].bitcast(I32),
                 in_=bs_rows[:, q : 16 : 4, :].rearrange("k s w -> s k w"),
             )
-        nc.sync.dma_start(out=amp_b[:], in_=amp.rearrange("(g p t) -> p g t", p=P, t=T))
         load_a(1)
+        load_a(2)
         load_bw(1)
         load_xb(1)
-        load_xa(1)
-        load_a(2)
-        load_bw(2)
         load_a(3)
+        load_bw(2)
+        load_xa(1)
         load_bw(3)
+        nc.sync.dma_start(out=amp_b[:], in_=amp.rearrange("(g p t) -> p g t", p=P, t=T))
         nc.sync.dma_start(out=cw[:].bitcast(I32), in_=cw_rows)
         for q in range(4):
             nc.sync.dma_start(
@@ -164,11 +154,10 @@ def tile_projection_pursuit_responses_s3_kernel(
             )
 
         def permw(g):
-            for k in range(KPB):
-                nc.vector.tensor_copy(
-                    out=live["bw", g][:, k, :].rearrange("p (t q b) -> p t q b", t=T, b=2),
-                    in_=bw_raw[g][:, k, :].rearrange("p (q t b) -> p t q b", t=T, b=2),
-                )
+            nc.vector.tensor_copy(
+                out=live["bw", g][:].rearrange("p k (t q b) -> p k t q b", t=T, b=2),
+                in_=bw_raw[g][:].rearrange("p k (q t b) -> p k t q b", t=T, b=2),
+            )
 
         def perms(g):
             nc.vector.tensor_copy(
@@ -239,7 +228,7 @@ def tile_projection_pursuit_responses_s3_kernel(
             for k in range(KPB):
                 quantize(f"xb{r}{k}", live["gx", r][:, k, :])
 
-        def project(r, g, t):
+        def lead(r, g, t):
             cols = slice(t * P, (t + 1) * P)
             z = zpool.tile([P, W], F32, name="z")
             live["z", r, g, t] = z
@@ -252,6 +241,10 @@ def tile_projection_pursuit_responses_s3_kernel(
                 start=True,
                 stop=False,
             )
+
+        def rest(r, g, t):
+            cols = slice(t * P, (t + 1) * P)
+            z = live["z", r, g, t]
             for k in range(KPB):
                 nc.tensor.matmul_mx(
                     out=z[:],
@@ -268,34 +261,23 @@ def tile_projection_pursuit_responses_s3_kernel(
                 live["th", r, g] = work.tile([P, T, W], F32, name="th")
             nc.scalar.activation(out=live["th", r, g][:, t, :], in_=live["z", r, g, t][:], func=TANH)
 
-        def smul(r, g, t):
-            if ("hp", r, g) not in live:
-                live["hp", r, g] = work.tile([P, T, W], BF16, name="hp")
-            nc.scalar.activation(
-                out=live["hp", r, g][:, t, :], in_=live["th", r, g][:, t, :], func=COPY, scale=amp_f[:, g, t, 0:1]
+        def mul(r, g, lo=0, hi=W):
+            if ("hb", r, g) not in live:
+                live["hb", r, g] = work.tile([P, W, T], BF16, align_bytes=64, name="hb")
+            cols = slice(lo, hi)
+            nc.vector.tensor_tensor(
+                out=live["hb", r, g][:, cols, :].rearrange("p (c i) t -> p c t i", i=4),
+                in0=live["th", r, g][:, :, cols].rearrange("p t (c i) -> p c t i", i=4),
+                in1=amp_f[:, g, :, :].unsqueeze(1).to_broadcast([P, (hi - lo) // 4, T, 4]),
+                op=MULT,
             )
 
-        def mul(r, g, h):
-            if h == 0:
-                live["hb", r, g] = work.tile([P, W, T], BF16, align_bytes=64, name="hb")
-            cols = slice(h * HALF, (h + 1) * HALF)
-            dst = live["hb", r, g][:, cols, :].rearrange("p (c i) t -> p c t i", i=4)
-            if (r, g) in SCALAR_UNITS:
-                nc.vector.tensor_copy(out=dst, in_=live["hp", r, g][:, :, cols].rearrange("p t (c i) -> p c t i", i=4))
-            else:
-                nc.vector.tensor_tensor(
-                    out=dst,
-                    in0=live["th", r, g][:, :, cols].rearrange("p t (c i) -> p c t i", i=4),
-                    in1=amp_f[:, g, :, :].unsqueeze(1).to_broadcast([P, HALF // 4, T, 4]),
-                    op=MULT,
-                )
-
-        def qh(r, g, h):
+        def qh(r, g, lo=0, hi=W):
             key = f"h{r}{g}"
-            if h == 0:
+            if key not in codes:
                 codes[key] = keep.tile([P, W], U32, align_bytes=64, name=key + "_codes")
                 scales[key] = keep.tile([P, W], U8, align_bytes=64, name=key + "_scales")
-            cols = slice(h * HALF, (h + 1) * HALF)
+            cols = slice(lo, hi)
             nc.vector.quantize_mx(
                 out=codes[key][:, cols].bitcast(FP8X4),
                 scales=scales[key][:, cols],
@@ -328,6 +310,13 @@ def tile_projection_pursuit_responses_s3_kernel(
             nc.vector.tensor_tensor(out=ysb[:], in0=live["y", r, j][:], in1=mean_sb[:], op=ADD)
             nc.sync.dma_start(out=out_rows[r][:, j, :], in_=ysb[:])
 
+        def early(r, j):
+            for g in range(GROUPS - 1):
+                respond(r, j, g)
+
+        def last(r, j):
+            respond(r, j, GROUPS - 1)
+
         table = {}
         for h in range(2):
             table[f"trs{h}"] = (trs, h)
@@ -347,15 +336,18 @@ def tile_projection_pursuit_responses_s3_kernel(
                 table[f"trxb{r}{j}"] = (trxb, r, j)
                 table[f"cpxb{r}{j}"] = (cpxb, r, j)
                 table[f"mean{r}{j}"] = (add_mean, r, j)
+                table[f"YE{r}{j}"] = (early, r, j)
+                table[f"YL{r}{j}"] = (last, r, j)
                 for g in range(GROUPS):
-                    table[f"Y{r}{j}.{g}"] = (respond, r, j, g)
-                    table[f"Z{r}{g}.{j}"] = (project, r, g, j)
+                    table[f"L{r}{g}.{j}"] = (lead, r, g, j)
+                    table[f"Z{r}{g}.{j}"] = (rest, r, g, j)
                     table[f"tanh{r}{g}.{j}"] = (tanh, r, g, j)
-                    table[f"smul{r}{g}.{j}"] = (smul, r, g, j)
             for g in range(GROUPS):
+                table[f"mul{r}{g}"] = (mul, r, g)
+                table[f"qh{r}{g}"] = (qh, r, g)
                 for h in range(2):
-                    table[f"mul{r}{g}.{h}"] = (mul, r, g, h)
-                    table[f"qh{r}{g}.{h}"] = (qh, r, g, h)
+                    table[f"mul{r}{g}.{h}"] = (mul, r, g, h * HALF, (h + 1) * HALF)
+                    table[f"qh{r}{g}.{h}"] = (qh, r, g, h * HALF, (h + 1) * HALF)
         with tc.manual_schedule():
             for name in SEQ.split():
                 job = table[name]

@@ -21,32 +21,14 @@ TANH = mybir.ActivationFunctionType.Tanh
 
 P = 128
 T = 4
-SEQ = """
-permw0 trs0 cps0 trs1 cps1 tra0.0 cpa0.0 tra0.1 cpa0.1 trxa0.0 cpxa0.0 trxa0.1
-cpxa0.1 deq00 trxb00 cpxb00 deq01 deq02 trxb01 cpxb01 deq03 trxb02 cpxb02 trxb03
-cpxb03 perms0 tra2.0 cpa2.0 tra2.1 cpa2.1 tra1.0 cpa1.0 tra1.1 cpa1.1 qa0 perms1
-tra3.0 cpa3.0 qxa0 deq10 qxb0 trxb10 cpxb10 L00.0 L00.1 L00.2 L00.3 tra3.1
-cpa3.1 deq11 trxb11 cpxb11 permw1 qa1 Z00.0 tanh00.0 Z00.1 tanh00.1 perms2 qa2
-deq12 qa3 Z00.2 tanh00.2 Z00.3 tanh00.3 L01.0 Z01.0 tanh01.0 L01.1 Z01.1 tanh01.1
-permw2 L01.2 Z01.2 tanh01.2 L01.3 Z01.3 tanh01.3 trxa1.0 cpxa1.0 trxa1.1 cpxa1.1 permw3
-perms3 mul00 deq13 L02.0 Z02.0 tanh02.0 L02.1 Z02.1 tanh02.1 L02.2 Z02.2 tanh02.2
-L02.3 Z02.3 tanh02.3 qxa1 trxb12 cpxb12 trxb13 cpxb13 mul01 qxb1 mul02 L03.0
-Z03.0 tanh03.0 L03.1 Z03.1 tanh03.1 L03.2 Z03.2 tanh03.2 L03.3 Z03.3 tanh03.3 qh00
-mul03 L10.0 Z10.0 tanh10.0 L10.1 Z10.1 tanh10.1 L10.2 Z10.2 tanh10.2 L10.3 Z10.3
-tanh10.3 qh02 L11.0 Z11.0 tanh11.0 L11.1 Z11.1 tanh11.1 L11.2 Z11.2 tanh11.2 L11.3
-Z11.3 tanh11.3 qh03 mul10 qh01 qh10 L12.0 Z12.0 tanh12.0 L12.1 Z12.1 tanh12.1
-L12.2 Z12.2 tanh12.2 L12.3 Z12.3 tanh12.3 mul11 YE00 L13.0 Z13.0 tanh13.0 L13.1
-Z13.1 tanh13.1 L13.2 Z13.2 tanh13.2 L13.3 Z13.3 tanh13.3 YL00 mul12 qh11 qh12
-YE01 YL01 YE02 YL02 mean00 mean01 mul13.0 mean02 qh13.0 YE03 YL03 mean03
-mul13.1 qh13.1 YE10 YL10 mean10 YE11 YL11 mean11 YE12 YL12 mean12 YE13
-YL13
-mean13
-"""
-W = 512
-HALF = W // 2
+W = P * T
 GROUPS = D // W
-RANGES = M // W
-KPB = KB // W
+HALVES = M // W
+KB_PASSES = KB // W
+WORDS = W // 2
+SCALES_ROW = KB // P
+NEAR = 4
+LAST = (HALVES - 1, GROUPS - 1)
 
 
 def tile_projection_pursuit_responses_s3_kernel(
@@ -56,299 +38,328 @@ def tile_projection_pursuit_responses_s3_kernel(
     with ExitStack() as ctx:
         keep = ctx.enter_context(tc.tile_pool(name="keep", bufs=1))
         work = ctx.enter_context(tc.tile_pool(name="work", bufs=4))
-        zpool = ctx.enter_context(tc.psum_pool(name="zpool", bufs=4))
-        tpool = ctx.enter_context(tc.psum_pool(name="tpool", bufs=2))
-        ypool = ctx.enter_context(tc.psum_pool(name="ypool", bufs=2))
+        z_banks = ctx.enter_context(tc.psum_pool(name="z_banks", bufs=4))
+        turn_banks = ctx.enter_context(tc.psum_pool(name="turn_banks", bufs=2))
+        y_banks = ctx.enter_context(tc.psum_pool(name="y_banks", bufs=2))
+
+        scale_cols = keep.tile([P, SCALES_ROW], F32, name="scale_cols")
+        amp_raw = keep.tile([P, GROUPS, T], BF16, name="amp_raw")
+        mean_row = keep.tile([P, R], BF16, name="mean_row")
+        b_scales_raw = keep.tile([P, KB_PASSES, D], U8, name="b_scales_raw")
+        c_scales_sb = keep.tile([P, GROUPS, R], U8, align_bytes=64, name="c_scales_sb")
+        c_words_sb = keep.tile([P, GROUPS, 2 * R], U8, align_bytes=64, name="c_words_sb")
+        b_words_raw = [keep.tile([P, KB_PASSES, 2 * W], U8, name=f"b_words_raw{g}") for g in range(GROUPS)]
+        a_raw = [keep.tile([P, T, KA], BF16, name=f"a_raw{g}") for g in range(GROUPS)]
+        xa_raw = [keep.tile([P, T, KA], BF16, name=f"xa_raw{s}") for s in range(HALVES)]
+        xb_raw = [keep.tile([P, T, KB], U8, name=f"xb_raw{s}") for s in range(HALVES)]
 
         a_rows = a.rearrange("(g p t) k -> g p t k", p=P, t=T)
-        xa_rows = xa.rearrange("(r p j) k -> r p j k", p=P, j=T)
-        xb_rows = xb_bytes.rearrange("(r p j) k -> r p j k", p=P, j=T)
-        out_rows = out.rearrange("(r p j) c -> r p j c", p=P, j=T)
-        bw_rows = b_words.bitcast(I32).rearrange("k p w -> p k w")
-        bs_rows = b_scales.bitcast(I32)
-        cw_rows = c_words.bitcast(I32).rearrange("k p w -> p k w")
-        cs_rows = c_scales.bitcast(I32)
+        xa_rows = xa.rearrange("(s p j) k -> s p j k", p=P, j=T)
+        xb_rows = xb_bytes.rearrange("(s p j) k -> s p j k", p=P, j=T)
+        out_rows = out.rearrange("(s p j) c -> s p j c", p=P, j=T)
+        b_words_rows = b_words.bitcast(I32).rearrange("k p w -> p k w")
 
-        scale_cols = keep.tile([P, 8], F32, name="scale_cols")
-        amp_b = keep.tile([P, GROUPS, T], BF16, name="amp_b")
-        amp_f = keep.tile([P, GROUPS, T, 4], F32, name="amp_f")
-        mean_sb = keep.tile([P, R], BF16, name="mean_sb")
-        bs_raw = keep.tile([P, KPB, D], U8, name="bs_raw")
-        cs = keep.tile([P, GROUPS, R], U8, align_bytes=64, name="cs")
-        cw = keep.tile([P, GROUPS, 2 * R], U8, align_bytes=64, name="cw")
-        bw_raw = [keep.tile([P, KPB, 2 * W], U8, name=f"bw_raw{g}") for g in range(GROUPS)]
-        a_raw = [keep.tile([P, T, KA], BF16, name=f"a_raw{g}") for g in range(GROUPS)]
-        xa_raw = [keep.tile([P, T, KA], BF16, name=f"xa_raw{r}") for r in range(RANGES)]
-        xb_raw = [keep.tile([P, T, KB], U8, name=f"xb_raw{r}") for r in range(RANGES)]
-
-        def load_bw(g):
-            nc.sync.dma_start(out=bw_raw[g][:].bitcast(I32), in_=bw_rows[:, :, g * 256 : (g + 1) * 256])
-
-        def load_a(g):
-            nc.sync.dma_start(out=a_raw[g][:], in_=a_rows[g])
-
-        def load_xa(r):
-            nc.sync.dma_start(out=xa_raw[r][:], in_=xa_rows[r])
-
-        def load_xb(r):
-            nc.sync.dma_start(out=xb_raw[r][:], in_=xb_rows[r])
-
-        nc.vector.memset(bs_raw[:].bitcast(I32), 0)
-        nc.gpsimd.memset(cs[:].bitcast(I32), 0)
-        nc.sync.dma_start(out=scale_cols[:], in_=xb_scale.rearrange("o (n m) -> n (o m)", m=8))
-        load_bw(0)
-        load_xb(0)
-        load_a(0)
-        load_xa(0)
-        for q in range(4):
+        def load_b_words(g):
             nc.sync.dma_start(
-                out=bs_raw[q : P : 32].bitcast(I32),
-                in_=bs_rows[:, q : 16 : 4, :].rearrange("k s w -> s k w"),
+                out=b_words_raw[g][:].bitcast(I32), in_=b_words_rows[:, :, g * WORDS : (g + 1) * WORDS]
             )
-        load_a(1)
-        load_a(2)
-        load_bw(1)
-        load_xb(1)
-        load_a(3)
-        load_bw(2)
-        load_xa(1)
-        load_bw(3)
-        nc.sync.dma_start(out=amp_b[:], in_=amp.rearrange("(g p t) -> p g t", p=P, t=T))
-        nc.sync.dma_start(out=cw[:].bitcast(I32), in_=cw_rows)
-        for q in range(4):
-            nc.sync.dma_start(
-                out=cs[q : P : 32].bitcast(I32),
-                in_=cs_rows[:, q : 16 : 4, :].rearrange("k s w -> s k w"),
-            )
-        nc.sync.dma_start(out=mean_sb[:], in_=mean.partition_broadcast(P))
+
+        def load_scale_bytes(tile, source):
+            rows = source.bitcast(I32)
+            for i in range(T):
+                nc.sync.dma_start(
+                    out=tile[i:P:32].bitcast(I32), in_=rows[:, i : 4 * T : T, :].rearrange("k q w -> q k w")
+                )
+
+        nc.vector.memset(b_scales_raw[:].bitcast(I32), 0)
+        nc.gpsimd.memset(c_scales_sb[:].bitcast(I32), 0)
+
+        nc.sync.dma_start(out=scale_cols[:], in_=xb_scale.rearrange("o (n m) -> n (o m)", m=SCALES_ROW))
+        load_b_words(0)
+        nc.sync.dma_start(out=xb_raw[0][:], in_=xb_rows[0])
+        nc.sync.dma_start(out=a_raw[0][:], in_=a_rows[0])
+        nc.sync.dma_start(out=xa_raw[0][:], in_=xa_rows[0])
+        load_scale_bytes(b_scales_raw, b_scales)
+        nc.sync.dma_start(out=a_raw[1][:], in_=a_rows[1])
+        nc.sync.dma_start(out=a_raw[2][:], in_=a_rows[2])
+        load_b_words(1)
+        nc.sync.dma_start(out=xb_raw[1][:], in_=xb_rows[1])
+        nc.sync.dma_start(out=a_raw[3][:], in_=a_rows[3])
+        load_b_words(2)
+        nc.sync.dma_start(out=xa_raw[1][:], in_=xa_rows[1])
+        load_b_words(3)
+        nc.sync.dma_start(out=amp_raw[:], in_=amp.rearrange("(g p t) -> p g t", p=P, t=T))
+        nc.sync.dma_start(out=c_words_sb[:].bitcast(I32), in_=c_words.bitcast(I32).rearrange("k p w -> p k w"))
+        load_scale_bytes(c_scales_sb, c_scales)
+        nc.sync.dma_start(out=mean_row[:], in_=mean.partition_broadcast(P))
 
         ident = keep.tile([P, P], F32, name="ident")
         make_identity(nc, ident[:])
-        warm = keep.tile([P, 1], F32, name="warm")
-        nc.vector.memset(warm[:], 0.0)
-        warm_out = keep.tile([P, 1], F32, name="warm_out")
-        nc.scalar.activation(out=warm_out[:], in_=warm[:], func=TANH)
 
-        scale_rows = keep.tile([P, KB], F32, name="scale_rows")
-        nc.vector.tensor_copy(out=amp_f[:], in_=amp_b[:].unsqueeze(3).to_broadcast([P, GROUPS, T, 4]))
-        live = {}
+        dummy = keep.tile([P, 1], F32, name="dummy")
+        nc.vector.memset(dummy[:], 0.0)
+        dummy_tanh = keep.tile([P, 1], F32, name="dummy_tanh")
+        nc.scalar.activation(out=dummy_tanh[:], in_=dummy[:], func=TANH)
+
+        amp_near = keep.tile([P, GROUPS, T, NEAR], F32, name="amp_near")
+        nc.gpsimd.tensor_copy(out=amp_near[:], in_=amp_raw[:].unsqueeze(3).to_broadcast([P, GROUPS, T, NEAR]))
+
+        scale_row = keep.tile([P, KB], F32, name="scale_row")
+        b_words_moved = [
+            keep.tile([P, KB_PASSES, 2 * W], U8, align_bytes=64, name=f"b_words_moved{g}") for g in range(GROUPS)
+        ]
+        b_scales_moved = [
+            keep.tile([P, KB_PASSES, W], U8, align_bytes=64, name=f"b_scales_moved{g}") for g in range(GROUPS)
+        ]
         codes = {}
         scales = {}
-        for g in range(GROUPS):
-            live["bw", g] = keep.tile([P, KPB, 2 * W], U8, align_bytes=64, name=f"bw{g}")
-            live["bs", g] = keep.tile([P, KPB, W], U8, align_bytes=64, name=f"bs{g}")
+        grouped = {}
+        widened = {}
+        z_open = {}
+        tanhs = {}
+        scaled = {}
+        ridges = {}
 
-        def trs(h):
-            live["sp", h] = tpool.tile([P, W], F32, name="tr")
-            for m in range(4):
-                nc.tensor.transpose(
-                    live["sp", h][:, m * P : (m + 1) * P],
-                    scale_cols[:, 4 * h + m : 4 * h + m + 1].to_broadcast([P, P]),
-                    ident[:],
-                )
-
-        def cps(h):
+        def spread_scales(h):
+            bank = turn_banks.tile([P, W], F32, name="turn")
+            for m in range(T):
+                col = scale_cols[:, T * h + m : T * h + m + 1]
+                nc.tensor.transpose(bank[:, m * P : (m + 1) * P], col.to_broadcast([P, P]), ident[:])
             nc.scalar.copy(
-                out=scale_rows[:].rearrange("p (n m) -> p n m", m=8)[:, :, 4 * h : 4 * h + 4],
-                in_=live["sp", h][:].rearrange("p (m n) -> p n m", m=4),
+                out=scale_row[:].rearrange("p (n m) -> p n m", m=SCALES_ROW)[:, :, T * h : T * (h + 1)],
+                in_=bank[:].rearrange("p (m n) -> p n m", m=T),
             )
 
-        def permw(g):
+        def move_b_words(g):
             nc.vector.tensor_copy(
-                out=live["bw", g][:].rearrange("p k (t q b) -> p k t q b", t=T, b=2),
-                in_=bw_raw[g][:].rearrange("p k (q t b) -> p k t q b", t=T, b=2),
+                out=b_words_moved[g][:].rearrange("p k (t q b) -> p k t q b", t=T, b=2),
+                in_=b_words_raw[g][:].rearrange("p k (q t b) -> p k t q b", t=T, b=2),
             )
 
-        def perms(g):
+        def move_b_scales(g):
             nc.vector.tensor_copy(
-                out=live["bs", g][:].rearrange("p k (t q) -> p k t q", t=T),
-                in_=bs_raw[:, :, g * W : (g + 1) * W].rearrange("p k (q t) -> p k t q", t=T),
+                out=b_scales_moved[g][:].rearrange("p k (t q) -> p k t q", t=T),
+                in_=b_scales_raw[:, :, g * W : (g + 1) * W].rearrange("p k (q t) -> p k t q", t=T),
             )
 
-        def quantize(key, grouped):
-            codes[key] = keep.tile([P, W], U32, align_bytes=64, name=key + "_codes")
-            scales[key] = keep.tile([P, W], U8, align_bytes=64, name=key + "_scales")
-            nc.vector.quantize_mx(out=codes[key][:].bitcast(FP8X4), scales=scales[key][:], in_=grouped)
+        def quantize(name, source, lo=0, hi=W):
+            if name not in codes:
+                codes[name] = keep.tile([P, W], U32, align_bytes=64, name=name + "_codes")
+                scales[name] = keep.tile([P, W], U8, align_bytes=64, name=name + "_scales")
+            nc.vector.quantize_mx(
+                out=codes[name][:, lo:hi].bitcast(FP8X4), scales=scales[name][:, lo:hi], in_=source[:, T * lo : T * hi]
+            )
 
-        raws = {}
-        for g in range(GROUPS):
-            raws[f"a{g}"] = a_raw[g]
-        for r in range(RANGES):
-            raws[f"xa{r}"] = xa_raw[r]
-
-        def tr_rows(key, pair):
-            words = raws[key][:].rearrange("p s k -> p (s k)").bitcast(F32)
-            live["tr", key, pair] = tpool.tile([P, W], F32, name="tr")
-            for s in range(2):
+        def turn_rows(name, raw, pair):
+            if name not in grouped:
+                grouped[name] = work.tile([P, W * T], BF16, align_bytes=64, name="grouped")
+            words = raw[:].rearrange("p j k -> p (j k)").bitcast(F32)
+            bank = turn_banks.tile([P, W], F32, name="turn")
+            for j in range(2):
                 for u in range(2):
-                    c = (2 * pair + s) * 256
-                    o = (2 * s + u) * P
-                    nc.tensor.transpose(
-                        live["tr", key, pair][:, o : o + P], words[:, c + u : c + 256 : 2], ident[:]
-                    )
-
-        def cp_rows(key, pair):
-            if ("grouped", key) not in live:
-                live["grouped", key] = work.tile([P, W, T], BF16, align_bytes=64, name="grouped")
-            gw = live["grouped", key][:].rearrange("p n t -> p (n t)").bitcast(F32)
+                    first = (2 * pair + j) * WORDS
+                    to = (2 * j + u) * P
+                    nc.tensor.transpose(bank[:, to : to + P], words[:, first + u : first + WORDS : 2], ident[:])
             nc.scalar.copy(
-                out=gw[:, pair * 512 : (pair + 1) * 512].rearrange("p (s r u) -> p s r u", s=2, u=2),
-                in_=live["tr", key, pair][:].rearrange("p (s u r) -> p s r u", s=2, u=2),
+                out=grouped[name][:].bitcast(F32)[:, pair * W : (pair + 1) * W].rearrange(
+                    "p (j r u) -> p j r u", j=2, u=2
+                ),
+                in_=bank[:].rearrange("p (j u r) -> p j r u", j=2, u=2),
             )
 
-        def q_rows(key):
-            quantize(key, live["grouped", key][:].rearrange("p n t -> p (n t)"))
+        def turn_a(g):
+            for pair in range(2):
+                turn_rows(f"a{g}", a_raw[g], pair)
 
-        def deq(r, j):
-            live["val", r, j] = work.tile([P, KB], BF16, name="xb_val")
+        def quantize_a(g):
+            quantize(f"a{g}", grouped[f"a{g}"][:])
+
+        def quantize_xa(s):
+            quantize(f"xa{s}", grouped[f"xa{s}"][:])
+
+        def widen_xb(s, j):
+            widened[s, j] = work.tile([P, KB], BF16, name="widened")
             nc.vector.tensor_tensor(
-                out=live["val", r, j][:], in0=xb_raw[r][:, j, :].bitcast(FP8), in1=scale_rows[:], op=MULT
+                out=widened[s, j][:], in0=xb_raw[s][:, j, :].bitcast(FP8), in1=scale_row[:], op=MULT
             )
 
-        def trxb(r, j):
-            words = live["val", r, j][:].bitcast(F32)
-            live["trx", r, j] = tpool.tile([P, W], F32, name="tr")
-            for k in range(KPB):
+        def turn_xb(s, j):
+            name = f"xb{s}"
+            if name not in grouped:
+                grouped[name] = work.tile([P, KB_PASSES * W * T], BF16, align_bytes=64, name="grouped_xb", bufs=2)
+            words = widened[s, j][:].bitcast(F32)
+            bank = turn_banks.tile([P, W], F32, name="turn")
+            for k in range(KB_PASSES):
                 for u in range(2):
-                    o = (2 * k + u) * P
+                    to = (2 * k + u) * P
                     nc.tensor.transpose(
-                        live["trx", r, j][:, o : o + P], words[:, 256 * k + u : 256 * (k + 1) : 2], ident[:]
+                        bank[:, to : to + P], words[:, k * WORDS + u : (k + 1) * WORDS : 2], ident[:]
                     )
-
-        def cpxb(r, j):
-            if ("gx", r) not in live:
-                live["gx", r] = work.tile([P, KPB, W * T], BF16, align_bytes=64, name="grouped_xb")
-            gw = live["gx", r][:].rearrange("p k n -> p (k n)").bitcast(F32).rearrange("p (k n) -> p k n", k=KPB)
+            by_pass = grouped[name][:].bitcast(F32).rearrange("p (k n) -> p k n", k=KB_PASSES)
             nc.scalar.copy(
-                out=gw[:, :, j * 256 : (j + 1) * 256].rearrange("p k (r u) -> p k r u", u=2),
-                in_=live["trx", r, j][:].rearrange("p (k u r) -> p k r u", k=KPB, u=2),
+                out=by_pass[:, :, j * WORDS : (j + 1) * WORDS].rearrange("p k (r u) -> p k r u", u=2),
+                in_=bank[:].rearrange("p (k u r) -> p k r u", k=KB_PASSES, u=2),
             )
 
-        def qxb(r):
-            for k in range(KPB):
-                quantize(f"xb{r}{k}", live["gx", r][:, k, :])
+        def quantize_xb(s):
+            for k in range(KB_PASSES):
+                quantize(f"xb{s}_{k}", grouped[f"xb{s}"][:, k * W * T : (k + 1) * W * T])
 
-        def lead(r, g, t):
+        def lead(s, g, t):
             cols = slice(t * P, (t + 1) * P)
-            z = zpool.tile([P, W], F32, name="z")
-            live["z", r, g, t] = z
+            z_open[s, g, t] = z_banks.tile([P, W], F32, name="z")
             nc.tensor.matmul_mx(
-                out=z[:],
+                out=z_open[s, g, t][:],
                 lhsT=codes[f"a{g}"][:, cols].bitcast(FP8X4),
                 lhsT_scale=scales[f"a{g}"][:, cols],
-                rhs=codes[f"xa{r}"][:].bitcast(FP8X4),
-                rhs_scale=scales[f"xa{r}"][:],
+                rhs=codes[f"xa{s}"][:].bitcast(FP8X4),
+                rhs_scale=scales[f"xa{s}"][:],
                 start=True,
                 stop=False,
             )
 
-        def rest(r, g, t):
+        def rest_and_tanh(s, g, t):
             cols = slice(t * P, (t + 1) * P)
-            z = live["z", r, g, t]
-            for k in range(KPB):
+            z = z_open[s, g, t]
+            for k in range(KB_PASSES):
                 nc.tensor.matmul_mx(
                     out=z[:],
-                    lhsT=live["bw", g][:, k, t * 256 : (t + 1) * 256].bitcast(FP4X4),
-                    lhsT_scale=live["bs", g][:, k, cols],
-                    rhs=codes[f"xb{r}{k}"][:].bitcast(FP8X4),
-                    rhs_scale=scales[f"xb{r}{k}"][:],
+                    lhsT=b_words_moved[g][:, k, 2 * t * P : 2 * (t + 1) * P].bitcast(FP4X4),
+                    lhsT_scale=b_scales_moved[g][:, k, cols],
+                    rhs=codes[f"xb{s}_{k}"][:].bitcast(FP8X4),
+                    rhs_scale=scales[f"xb{s}_{k}"][:],
                     start=False,
-                    stop=(k == KPB - 1),
+                    stop=(k == KB_PASSES - 1),
                 )
+            if (s, g) not in tanhs:
+                tanhs[s, g] = work.tile([P, T, W], F32, name="tanh")
+            nc.scalar.activation(out=tanhs[s, g][:, t, :], in_=z[:], func=TANH)
 
-        def tanh(r, g, t):
-            if ("th", r, g) not in live:
-                live["th", r, g] = work.tile([P, T, W], F32, name="th")
-            nc.scalar.activation(out=live["th", r, g][:, t, :], in_=live["z", r, g, t][:], func=TANH)
+        def project(s, g, slots=range(T)):
+            for t in slots:
+                lead(s, g, t)
+                rest_and_tanh(s, g, t)
 
-        def mul(r, g, lo=0, hi=W):
-            if ("hb", r, g) not in live:
-                live["hb", r, g] = work.tile([P, W, T], BF16, align_bytes=64, name="hb")
-            cols = slice(lo, hi)
+        def interleaved(s, g, lo, hi):
+            if (s, g) not in ridges:
+                ridges[s, g] = work.tile([P, W, T], BF16, align_bytes=64, name="ridge")
+            return ridges[s, g][:, lo:hi, :].rearrange("p (c i) t -> p c t i", i=NEAR)
+
+        def multiply(s, g):
             nc.vector.tensor_tensor(
-                out=live["hb", r, g][:, cols, :].rearrange("p (c i) t -> p c t i", i=4),
-                in0=live["th", r, g][:, :, cols].rearrange("p t (c i) -> p c t i", i=4),
-                in1=amp_f[:, g, :, :].unsqueeze(1).to_broadcast([P, (hi - lo) // 4, T, 4]),
+                out=interleaved(s, g, 0, W),
+                in0=tanhs[s, g][:].rearrange("p t (c i) -> p c t i", i=NEAR),
+                in1=amp_near[:, g, :, :].unsqueeze(1).to_broadcast([P, W // NEAR, T, NEAR]),
                 op=MULT,
             )
 
-        def qh(r, g, lo=0, hi=W):
-            key = f"h{r}{g}"
-            if key not in codes:
-                codes[key] = keep.tile([P, W], U32, align_bytes=64, name=key + "_codes")
-                scales[key] = keep.tile([P, W], U8, align_bytes=64, name=key + "_scales")
-            cols = slice(lo, hi)
-            nc.vector.quantize_mx(
-                out=codes[key][:, cols].bitcast(FP8X4),
-                scales=scales[key][:, cols],
-                in_=live["hb", r, g][:, cols, :].rearrange("p n t -> p (n t)"),
+        def quantize_h(s, g, lo=0, hi=W):
+            quantize(f"h{s}{g}", ridges[s, g][:].rearrange("p n t -> p (n t)"), lo, hi)
+
+        def multiply_on_scalar(s, g):
+            scaled[s, g] = keep.tile([P, T, W], BF16, name="scaled")
+            for t in range(T):
+                nc.scalar.activation(
+                    out=scaled[s, g][:, t, :], in_=tanhs[s, g][:, t, :], func=COPY, scale=amp_near[:, g, t, 0:1]
+                )
+
+        def interleave(s, g, lo, hi):
+            nc.vector.tensor_copy(
+                out=interleaved(s, g, lo, hi),
+                in_=scaled[s, g][:, :, lo:hi].rearrange("p t (c i) -> p c t i", i=NEAR),
             )
 
-        def respond(r, j, g):
-            if ("y", r, j) not in live:
-                if r == 1 and j >= 2:
-                    live["y", r, j] = tpool.tile([P, W], F32, name="tr")
-                else:
-                    live["y", r, j] = ypool.tile([P, W], F32, name="y")
-                live["n", r, j] = 0
-            key = f"h{r}{g}"
+        def respond(s, j):
             cols = slice(j * P, (j + 1) * P)
-            n = live["n", r, j]
-            nc.tensor.matmul_mx(
-                out=live["y", r, j][:],
-                lhsT=codes[key][:, cols].bitcast(FP8X4),
-                lhsT_scale=scales[key][:, cols],
-                rhs=cw[:, g, :].bitcast(FP4X4),
-                rhs_scale=cs[:, g, :],
-                start=(n == 0),
-                stop=(n == GROUPS - 1),
-            )
-            live["n", r, j] = n + 1
-
-        def add_mean(r, j):
-            ysb = work.tile([P, R], F32, name="ysb")
-            nc.vector.tensor_tensor(out=ysb[:], in0=live["y", r, j][:], in1=mean_sb[:], op=ADD)
-            nc.sync.dma_start(out=out_rows[r][:, j, :], in_=ysb[:])
-
-        def early(r, j):
-            for g in range(GROUPS - 1):
-                respond(r, j, g)
-
-        def last(r, j):
-            respond(r, j, GROUPS - 1)
-
-        table = {}
-        for h in range(2):
-            table[f"trs{h}"] = (trs, h)
-            table[f"cps{h}"] = (cps, h)
-        for g in range(GROUPS):
-            table[f"permw{g}"] = (permw, g)
-            table[f"perms{g}"] = (perms, g)
-        for key in raws:
-            for pair in range(2):
-                table[f"tr{key}.{pair}"] = (tr_rows, key, pair)
-                table[f"cp{key}.{pair}"] = (cp_rows, key, pair)
-            table[f"q{key}"] = (q_rows, key)
-        for r in range(RANGES):
-            table[f"qxb{r}"] = (qxb, r)
-            for j in range(T):
-                table[f"deq{r}{j}"] = (deq, r, j)
-                table[f"trxb{r}{j}"] = (trxb, r, j)
-                table[f"cpxb{r}{j}"] = (cpxb, r, j)
-                table[f"mean{r}{j}"] = (add_mean, r, j)
-                table[f"YE{r}{j}"] = (early, r, j)
-                table[f"YL{r}{j}"] = (last, r, j)
-                for g in range(GROUPS):
-                    table[f"L{r}{g}.{j}"] = (lead, r, g, j)
-                    table[f"Z{r}{g}.{j}"] = (rest, r, g, j)
-                    table[f"tanh{r}{g}.{j}"] = (tanh, r, g, j)
+            if s == LAST[0] and j >= 2:
+                y = turn_banks.tile([P, W], F32, name="turn")
+            else:
+                y = y_banks.tile([P, W], F32, name="y")
             for g in range(GROUPS):
-                table[f"mul{r}{g}"] = (mul, r, g)
-                table[f"qh{r}{g}"] = (qh, r, g)
-                for h in range(2):
-                    table[f"mul{r}{g}.{h}"] = (mul, r, g, h * HALF, (h + 1) * HALF)
-                    table[f"qh{r}{g}.{h}"] = (qh, r, g, h * HALF, (h + 1) * HALF)
+                nc.tensor.matmul_mx(
+                    out=y[:],
+                    lhsT=codes[f"h{s}{g}"][:, cols].bitcast(FP8X4),
+                    lhsT_scale=scales[f"h{s}{g}"][:, cols],
+                    rhs=c_words_sb[:, g, :].bitcast(FP4X4),
+                    rhs_scale=c_scales_sb[:, g, :],
+                    start=(g == 0),
+                    stop=(g == GROUPS - 1),
+                )
+            y_sb = work.tile([P, R], F32, name="y_sb")
+            nc.vector.tensor_tensor(out=y_sb[:], in0=y[:], in1=mean_row[:], op=ADD)
+            nc.sync.dma_start(out=out_rows[s][:, j, :], in_=y_sb[:])
+
         with tc.manual_schedule():
-            for name in SEQ.split():
-                job = table[name]
-                job[0](*job[1:])
+            move_b_words(0)
+            spread_scales(0)
+            spread_scales(1)
+            for j in range(T):
+                widen_xb(0, j)
+            turn_a(0)
+            turn_rows("xa0", xa_raw[0], 0)
+            turn_xb(0, 0)
+            turn_rows("xa0", xa_raw[0], 1)
+            quantize_xa(0)
+            quantize_a(0)
+            for j in range(1, T):
+                turn_xb(0, j)
+            turn_a(1)
+            move_b_scales(0)
+            widen_xb(1, 0)
+            for t in range(T):
+                lead(0, 0, t)
+            quantize_xb(0)
+
+            turn_a(2)
+            move_b_words(1)
+            move_b_scales(1)
+            quantize_a(1)
+            move_b_words(2)
+            for t in range(2):
+                rest_and_tanh(0, 0, t)
+            widen_xb(1, 1)
+            widen_xb(1, 2)
+            move_b_scales(2)
+            quantize_a(2)
+            widen_xb(1, 3)
+            turn_a(3)
+            for t in range(2, T):
+                rest_and_tanh(0, 0, t)
+            move_b_words(3)
+            move_b_scales(3)
+            quantize_a(3)
+            for pair in range(2):
+                turn_rows("xa1", xa_raw[1], pair)
+            project(0, 1)
+            quantize_xa(1)
+            turn_xb(1, 0)
+            turn_xb(1, 1)
+            project(0, 2, range(2))
+            turn_xb(1, 2)
+            multiply(0, 0)
+            turn_xb(1, 3)
+            project(0, 2, range(2, T))
+            quantize_xb(1)
+
+            done = [(s, g) for s in range(HALVES) for g in range(GROUPS)]
+            for i in range(1, 6):
+                project(*done[i + 2])
+                multiply(*done[i])
+                quantize_h(*done[i - 1])
+            multiply(*done[6])
+            quantize_h(*done[5])
+
+            part = W // 2
+            multiply_on_scalar(*LAST)
+            respond(0, 0)
+            respond(0, 1)
+            quantize_h(*done[6])
+            interleave(*LAST, 0, part)
+            respond(0, 2)
+            quantize_h(*LAST, 0, part)
+            respond(0, 3)
+            interleave(*LAST, part, W)
+            respond(1, 0)
+            quantize_h(*LAST, part, W)
+            for j in range(1, T):
+                respond(1, j)

from contextlib import ExitStack

import concourse.mybir as mybir
from concourse.masks import make_identity

M, KA, KB, D, R = 1024, 512, 1024, 2048, 512
FLOPS = 2 * M * D * (KA + KB) + 2 * M * D * R

F32 = mybir.dt.float32
BF16 = mybir.dt.bfloat16
I32 = mybir.dt.int32
U32 = mybir.dt.uint32
U8 = mybir.dt.uint8
FP8 = mybir.dt.float8_e4m3fn
FP8X4 = mybir.dt.float8_e4m3fn_x4
FP4X4 = mybir.dt.float4_e2m1fn_x4
MULT = mybir.AluOpType.mult
ADD = mybir.AluOpType.add
COPY = mybir.ActivationFunctionType.Copy
TANH = mybir.ActivationFunctionType.Tanh

P = 128
T = 4
W = P * T
GROUPS = D // W
HALVES = M // W
KB_PASSES = KB // W
WORDS = W // 2
SCALES_ROW = KB // P
NEAR = 4
LAST = (HALVES - 1, GROUPS - 1)


def tile_projection_pursuit_responses_s3_kernel(
    tc, xa, xb_bytes, xb_scale, a, b_words, b_scales, amp, c_words, c_scales, mean, out
):
    nc = tc.nc
    with ExitStack() as ctx:
        keep = ctx.enter_context(tc.tile_pool(name="keep", bufs=1))
        work = ctx.enter_context(tc.tile_pool(name="work", bufs=4))
        z_banks = ctx.enter_context(tc.psum_pool(name="z_banks", bufs=4))
        turn_banks = ctx.enter_context(tc.psum_pool(name="turn_banks", bufs=2))
        y_banks = ctx.enter_context(tc.psum_pool(name="y_banks", bufs=2))

        scale_cols = keep.tile([P, SCALES_ROW], F32, name="scale_cols")
        amp_raw = keep.tile([P, GROUPS, T], BF16, name="amp_raw")
        mean_row = keep.tile([P, R], BF16, name="mean_row")
        b_scales_raw = keep.tile([P, KB_PASSES, D], U8, name="b_scales_raw")
        c_scales_sb = keep.tile([P, GROUPS, R], U8, align_bytes=64, name="c_scales_sb")
        c_words_sb = keep.tile([P, GROUPS, 2 * R], U8, align_bytes=64, name="c_words_sb")
        b_words_raw = [keep.tile([P, KB_PASSES, 2 * W], U8, name=f"b_words_raw{g}") for g in range(GROUPS)]
        a_raw = [keep.tile([P, T, KA], BF16, name=f"a_raw{g}") for g in range(GROUPS)]
        xa_raw = [keep.tile([P, T, KA], BF16, name=f"xa_raw{s}") for s in range(HALVES)]
        xb_raw = [keep.tile([P, T, KB], U8, name=f"xb_raw{s}") for s in range(HALVES)]

        a_rows = a.rearrange("(g p t) k -> g p t k", p=P, t=T)
        xa_rows = xa.rearrange("(s p j) k -> s p j k", p=P, j=T)
        xb_rows = xb_bytes.rearrange("(s p j) k -> s p j k", p=P, j=T)
        out_rows = out.rearrange("(s p j) c -> s p j c", p=P, j=T)
        b_words_rows = b_words.bitcast(I32).rearrange("k p w -> p k w")

        def load_b_words(g):
            nc.sync.dma_start(
                out=b_words_raw[g][:].bitcast(I32), in_=b_words_rows[:, :, g * WORDS : (g + 1) * WORDS]
            )

        def load_scale_bytes(tile, source):
            rows = source.bitcast(I32)
            for i in range(T):
                nc.sync.dma_start(
                    out=tile[i:P:32].bitcast(I32), in_=rows[:, i : 4 * T : T, :].rearrange("k q w -> q k w")
                )

        nc.vector.memset(b_scales_raw[:].bitcast(I32), 0)
        nc.gpsimd.memset(c_scales_sb[:].bitcast(I32), 0)

        nc.sync.dma_start(out=scale_cols[:], in_=xb_scale.rearrange("o (n m) -> n (o m)", m=SCALES_ROW))
        load_b_words(0)
        nc.sync.dma_start(out=xb_raw[0][:], in_=xb_rows[0])
        nc.sync.dma_start(out=a_raw[0][:], in_=a_rows[0])
        nc.sync.dma_start(out=xa_raw[0][:], in_=xa_rows[0])
        load_scale_bytes(b_scales_raw, b_scales)
        nc.sync.dma_start(out=a_raw[1][:], in_=a_rows[1])
        nc.sync.dma_start(out=a_raw[2][:], in_=a_rows[2])
        load_b_words(1)
        nc.sync.dma_start(out=xb_raw[1][:], in_=xb_rows[1])
        nc.sync.dma_start(out=a_raw[3][:], in_=a_rows[3])
        load_b_words(2)
        nc.sync.dma_start(out=xa_raw[1][:], in_=xa_rows[1])
        load_b_words(3)
        nc.sync.dma_start(out=amp_raw[:], in_=amp.rearrange("(g p t) -> p g t", p=P, t=T))
        nc.sync.dma_start(out=c_words_sb[:].bitcast(I32), in_=c_words.bitcast(I32).rearrange("k p w -> p k w"))
        load_scale_bytes(c_scales_sb, c_scales)
        nc.sync.dma_start(out=mean_row[:], in_=mean.partition_broadcast(P))

        ident = keep.tile([P, P], F32, name="ident")
        make_identity(nc, ident[:])

        dummy = keep.tile([P, 1], F32, name="dummy")
        nc.vector.memset(dummy[:], 0.0)
        dummy_tanh = keep.tile([P, 1], F32, name="dummy_tanh")
        nc.scalar.activation(out=dummy_tanh[:], in_=dummy[:], func=TANH)

        amp_near = keep.tile([P, GROUPS, T, NEAR], F32, name="amp_near")
        nc.gpsimd.tensor_copy(out=amp_near[:], in_=amp_raw[:].unsqueeze(3).to_broadcast([P, GROUPS, T, NEAR]))

        scale_row = keep.tile([P, KB], F32, name="scale_row")
        b_words_moved = [
            keep.tile([P, KB_PASSES, 2 * W], U8, align_bytes=64, name=f"b_words_moved{g}") for g in range(GROUPS)
        ]
        b_scales_moved = [
            keep.tile([P, KB_PASSES, W], U8, align_bytes=64, name=f"b_scales_moved{g}") for g in range(GROUPS)
        ]
        codes = {}
        scales = {}
        grouped = {}
        widened = {}
        z_open = {}
        tanhs = {}
        scaled = {}
        ridges = {}

        def spread_scales(h):
            bank = turn_banks.tile([P, W], F32, name="turn")
            for m in range(T):
                col = scale_cols[:, T * h + m : T * h + m + 1]
                nc.tensor.transpose(bank[:, m * P : (m + 1) * P], col.to_broadcast([P, P]), ident[:])
            nc.scalar.copy(
                out=scale_row[:].rearrange("p (n m) -> p n m", m=SCALES_ROW)[:, :, T * h : T * (h + 1)],
                in_=bank[:].rearrange("p (m n) -> p n m", m=T),
            )

        def move_b_words(g):
            nc.vector.tensor_copy(
                out=b_words_moved[g][:].rearrange("p k (t q b) -> p k t q b", t=T, b=2),
                in_=b_words_raw[g][:].rearrange("p k (q t b) -> p k t q b", t=T, b=2),
            )

        def move_b_scales(g):
            nc.vector.tensor_copy(
                out=b_scales_moved[g][:].rearrange("p k (t q) -> p k t q", t=T),
                in_=b_scales_raw[:, :, g * W : (g + 1) * W].rearrange("p k (q t) -> p k t q", t=T),
            )

        def quantize(name, source, lo=0, hi=W):
            if name not in codes:
                codes[name] = keep.tile([P, W], U32, align_bytes=64, name=name + "_codes")
                scales[name] = keep.tile([P, W], U8, align_bytes=64, name=name + "_scales")
            nc.vector.quantize_mx(
                out=codes[name][:, lo:hi].bitcast(FP8X4), scales=scales[name][:, lo:hi], in_=source[:, T * lo : T * hi]
            )

        def turn_rows(name, raw, pair):
            if name not in grouped:
                grouped[name] = work.tile([P, W * T], BF16, align_bytes=64, name="grouped")
            words = raw[:].rearrange("p j k -> p (j k)").bitcast(F32)
            bank = turn_banks.tile([P, W], F32, name="turn")
            for j in range(2):
                for u in range(2):
                    first = (2 * pair + j) * WORDS
                    to = (2 * j + u) * P
                    nc.tensor.transpose(bank[:, to : to + P], words[:, first + u : first + WORDS : 2], ident[:])
            nc.scalar.copy(
                out=grouped[name][:].bitcast(F32)[:, pair * W : (pair + 1) * W].rearrange(
                    "p (j r u) -> p j r u", j=2, u=2
                ),
                in_=bank[:].rearrange("p (j u r) -> p j r u", j=2, u=2),
            )

        def turn_a(g):
            for pair in range(2):
                turn_rows(f"a{g}", a_raw[g], pair)

        def quantize_a(g):
            quantize(f"a{g}", grouped[f"a{g}"][:])

        def quantize_xa(s):
            quantize(f"xa{s}", grouped[f"xa{s}"][:])

        def widen_xb(s, j):
            widened[s, j] = work.tile([P, KB], BF16, name="widened")
            nc.vector.tensor_tensor(
                out=widened[s, j][:], in0=xb_raw[s][:, j, :].bitcast(FP8), in1=scale_row[:], op=MULT
            )

        def turn_xb(s, j):
            name = f"xb{s}"
            if name not in grouped:
                grouped[name] = work.tile([P, KB_PASSES * W * T], BF16, align_bytes=64, name="grouped_xb", bufs=2)
            words = widened[s, j][:].bitcast(F32)
            bank = turn_banks.tile([P, W], F32, name="turn")
            for k in range(KB_PASSES):
                for u in range(2):
                    to = (2 * k + u) * P
                    nc.tensor.transpose(
                        bank[:, to : to + P], words[:, k * WORDS + u : (k + 1) * WORDS : 2], ident[:]
                    )
            by_pass = grouped[name][:].bitcast(F32).rearrange("p (k n) -> p k n", k=KB_PASSES)
            nc.scalar.copy(
                out=by_pass[:, :, j * WORDS : (j + 1) * WORDS].rearrange("p k (r u) -> p k r u", u=2),
                in_=bank[:].rearrange("p (k u r) -> p k r u", k=KB_PASSES, u=2),
            )

        def quantize_xb(s):
            for k in range(KB_PASSES):
                quantize(f"xb{s}_{k}", grouped[f"xb{s}"][:, k * W * T : (k + 1) * W * T])

        def lead(s, g, t):
            cols = slice(t * P, (t + 1) * P)
            z_open[s, g, t] = z_banks.tile([P, W], F32, name="z")
            nc.tensor.matmul_mx(
                out=z_open[s, g, t][:],
                lhsT=codes[f"a{g}"][:, cols].bitcast(FP8X4),
                lhsT_scale=scales[f"a{g}"][:, cols],
                rhs=codes[f"xa{s}"][:].bitcast(FP8X4),
                rhs_scale=scales[f"xa{s}"][:],
                start=True,
                stop=False,
            )

        def rest_and_tanh(s, g, t):
            cols = slice(t * P, (t + 1) * P)
            z = z_open[s, g, t]
            for k in range(KB_PASSES):
                nc.tensor.matmul_mx(
                    out=z[:],
                    lhsT=b_words_moved[g][:, k, 2 * t * P : 2 * (t + 1) * P].bitcast(FP4X4),
                    lhsT_scale=b_scales_moved[g][:, k, cols],
                    rhs=codes[f"xb{s}_{k}"][:].bitcast(FP8X4),
                    rhs_scale=scales[f"xb{s}_{k}"][:],
                    start=False,
                    stop=(k == KB_PASSES - 1),
                )
            if (s, g) not in tanhs:
                tanhs[s, g] = work.tile([P, T, W], F32, name="tanh")
            nc.scalar.activation(out=tanhs[s, g][:, t, :], in_=z[:], func=TANH)

        def project(s, g, slots=range(T)):
            for t in slots:
                lead(s, g, t)
                rest_and_tanh(s, g, t)

        def interleaved(s, g, lo, hi):
            if (s, g) not in ridges:
                ridges[s, g] = work.tile([P, W, T], BF16, align_bytes=64, name="ridge")
            return ridges[s, g][:, lo:hi, :].rearrange("p (c i) t -> p c t i", i=NEAR)

        def multiply(s, g):
            nc.vector.tensor_tensor(
                out=interleaved(s, g, 0, W),
                in0=tanhs[s, g][:].rearrange("p t (c i) -> p c t i", i=NEAR),
                in1=amp_near[:, g, :, :].unsqueeze(1).to_broadcast([P, W // NEAR, T, NEAR]),
                op=MULT,
            )

        def quantize_h(s, g, lo=0, hi=W):
            quantize(f"h{s}{g}", ridges[s, g][:].rearrange("p n t -> p (n t)"), lo, hi)

        def multiply_on_scalar(s, g):
            scaled[s, g] = keep.tile([P, T, W], BF16, name="scaled")
            for t in range(T):
                nc.scalar.activation(
                    out=scaled[s, g][:, t, :], in_=tanhs[s, g][:, t, :], func=COPY, scale=amp_near[:, g, t, 0:1]
                )

        def interleave(s, g, lo, hi):
            nc.vector.tensor_copy(
                out=interleaved(s, g, lo, hi),
                in_=scaled[s, g][:, :, lo:hi].rearrange("p t (c i) -> p c t i", i=NEAR),
            )

        def respond(s, j):
            cols = slice(j * P, (j + 1) * P)
            if s == LAST[0] and j >= 2:
                y = turn_banks.tile([P, W], F32, name="turn")
            else:
                y = y_banks.tile([P, W], F32, name="y")
            for g in range(GROUPS):
                nc.tensor.matmul_mx(
                    out=y[:],
                    lhsT=codes[f"h{s}{g}"][:, cols].bitcast(FP8X4),
                    lhsT_scale=scales[f"h{s}{g}"][:, cols],
                    rhs=c_words_sb[:, g, :].bitcast(FP4X4),
                    rhs_scale=c_scales_sb[:, g, :],
                    start=(g == 0),
                    stop=(g == GROUPS - 1),
                )
            y_sb = work.tile([P, R], F32, name="y_sb")
            nc.vector.tensor_tensor(out=y_sb[:], in0=y[:], in1=mean_row[:], op=ADD)
            nc.sync.dma_start(out=out_rows[s][:, j, :], in_=y_sb[:])

        with tc.manual_schedule():
            move_b_words(0)
            spread_scales(0)
            spread_scales(1)
            for j in range(T):
                widen_xb(0, j)
            turn_a(0)
            turn_rows("xa0", xa_raw[0], 0)
            turn_xb(0, 0)
            turn_rows("xa0", xa_raw[0], 1)
            quantize_xa(0)
            quantize_a(0)
            for j in range(1, T):
                turn_xb(0, j)
            turn_a(1)
            move_b_scales(0)
            widen_xb(1, 0)
            for t in range(T):
                lead(0, 0, t)
            quantize_xb(0)

            turn_a(2)
            move_b_words(1)
            move_b_scales(1)
            quantize_a(1)
            move_b_words(2)
            for t in range(2):
                rest_and_tanh(0, 0, t)
            widen_xb(1, 1)
            widen_xb(1, 2)
            move_b_scales(2)
            quantize_a(2)
            widen_xb(1, 3)
            turn_a(3)
            for t in range(2, T):
                rest_and_tanh(0, 0, t)
            move_b_words(3)
            move_b_scales(3)
            quantize_a(3)
            for pair in range(2):
                turn_rows("xa1", xa_raw[1], pair)
            project(0, 1)
            quantize_xa(1)
            turn_xb(1, 0)
            turn_xb(1, 1)
            project(0, 2, range(2))
            turn_xb(1, 2)
            multiply(0, 0)
            turn_xb(1, 3)
            project(0, 2, range(2, T))
            quantize_xb(1)

            done = [(s, g) for s in range(HALVES) for g in range(GROUPS)]
            for i in range(1, 6):
                project(*done[i + 2])
                multiply(*done[i])
                quantize_h(*done[i - 1])
            multiply(*done[6])
            quantize_h(*done[5])

            part = W // 2
            multiply_on_scalar(*LAST)
            respond(0, 0)
            respond(0, 1)
            quantize_h(*done[6])
            interleave(*LAST, 0, part)
            respond(0, 2)
            quantize_h(*LAST, 0, part)
            respond(0, 3)
            interleave(*LAST, part, W)
            respond(1, 0)
            quantize_h(*LAST, part, W)
            for j in range(1, T):
                respond(1, j)
